import numpy as np
import ml_dtypes


def mxq(x, axis, fmt="e4m3"):
    dtype, down = {"e4m3": (ml_dtypes.float8_e4m3fn, 7), "e5m2": (ml_dtypes.float8_e5m2, 14)}[fmt]
    v = np.moveaxis(np.asarray(x, np.float32).astype(ml_dtypes.bfloat16).astype(np.float64), axis, -1)
    blocks = v.reshape(v.shape[:-1] + (-1, 32))
    amax = np.abs(blocks).max(-1, keepdims=True)
    byte = np.maximum(np.where(amax > 0, np.frexp(amax)[1] - 1 + 127, 0) - down, 1)
    scale = np.exp2(byte - 127.0)
    codes = (blocks / scale).astype(np.float32).astype(dtype).astype(np.float64)
    return np.moveaxis((codes * scale).reshape(v.shape), -1, axis)


WIDE = False


def mx_kscale(k):
    if not WIDE:
        return np.ones(k)
    levels = np.array([10, -10, 5, -5, 0])
    if k % 512:
        return np.exp2(np.random.permutation(np.resize(levels, k // 32))).repeat(32)
    a = np.empty((k // 512, 16))
    for p in range(k // 512):
        a[p, :8] = np.random.permutation(np.resize(levels, 8))
        for g in range(8):
            far = levels[np.abs(levels - a[p, g]) >= 10]
            a[p, g + 8] = far[np.random.randint(len(far))]
    return np.exp2(a.ravel()).repeat(32)


def f64(x):
    return np.asarray(x).astype(np.float64)


def striped(idx):
    return np.tile(idx.reshape(-1, 16).T, (8, 1)).astype(np.uint16)


def unstriped(offs):
    return offs[:16].T.reshape(-1).astype(np.int64)


def striped8(idx):
    return np.concatenate([x.reshape(-1, 16).T for x in idx]).astype(np.uint16)


def runs(offs, k):
    lists = np.stack([offs[16 * r : 16 * r + 16].T.reshape(-1) for r in range(8)]).astype(np.int64)
    return lists[np.arange(k) % 512 // 64]


def pack_weight(w):
    k, n = w.shape
    w = f64(np.asarray(w, np.float32).astype(ml_dtypes.bfloat16)).reshape(k // 32, 32, n)
    amax = np.abs(w).max(1)
    byte = np.clip(np.where(amax > 0, np.frexp(amax)[1] - 1 + 127 - 7, 1), 1, 254)
    scaled = (w * np.exp2(127.0 - byte)[:, None, :]).reshape(k, n).astype(np.float32)
    words = np.ascontiguousarray(scaled.reshape(k // 512, 128, 4, n).transpose(0, 1, 3, 2)).astype(ml_dtypes.float8_e4m3fn).view(np.uint8)
    return words, np.ascontiguousarray(byte.astype(np.uint8).reshape(k // 512, 16, n))


def unpack_weight(words, scales):
    g, p, n, _ = words.shape
    vals = np.ascontiguousarray(words).view(ml_dtypes.float8_e4m3fn).astype(np.float64) * np.repeat(np.exp2(scales.astype(np.float64) - 127.0), 8, axis=1)[..., None]
    return vals.transpose(0, 1, 3, 2).reshape(g * 512, n)


K, T, S, N, U, H = 512, 2048, 512, 512, 1024, 512


def setup_inputs():
    n = np.random.standard_normal
    s = mx_kscale(K)[:, None]
    u = mx_kscale(H)
    packed_xT = pack_weight(n((K, T)) * s)
    return {
        "x_words": packed_xT[0],
        "x_scales": packed_xT[1],
        "w1": (n((K, H)) / np.sqrt(K) / s * u).astype(np.float32),
        "w2": (n((H, N)) / np.sqrt(2 * H) / u[:, None]).astype(np.float32),
        "w3": (n((K, N)) / np.sqrt(2 * K) / s).astype(np.float32),
        "offs": striped(np.random.permutation(T)[:S]),
        "where": striped8(np.stack([np.random.permutation(U)[:S] for _ in range(8)])),
        "skip": striped(np.random.permutation(T)[:U]),
    }


def reference(x_words, x_scales, w1, w2, w3, offs, where, skip):
    xq = unpack_weight(x_words, x_scales)[:, unstriped(offs)]
    y = mxq(f64(w1), 0, "e4m3").T @ xq
    z = np.zeros((H, U))
    z[np.arange(H)[:, None], runs(where, H)] = y
    x_skip = unpack_weight(x_words, x_scales)[:, unstriped(skip)]
    return mxq(f64(w2), 0, "e4m3").T @ mxq(z, 0, "e4m3") + mxq(f64(w3), 0, "e4m3").T @ x_skip

@@ -1,0 +1,223 @@
+from contextlib import ExitStack
+
+import concourse.mybir as mybir
+
+K, T, S, N, U, H = 512, 2048, 512, 512, 1024, 512
+FLOPS = 2 * K * H * S + 2 * H * N * U + 2 * K * N * U
+
+F32 = mybir.dt.float32
+BF16 = mybir.dt.bfloat16
+I32 = mybir.dt.int32
+U32 = mybir.dt.uint32
+U16 = mybir.dt.uint16
+U8 = mybir.dt.uint8
+FP8X4 = mybir.dt.float8_e4m3fn_x4
+
+P = 128
+PACK = 4
+LIST_ROWS = 16
+HALF = S // 2
+CHUNK = 256
+ALIGN = 64
+VECTOR_SHARE = 160
+
+
+def entries(lst, first, count):
+    return lst[:, first // LIST_ROWS : (first + count) // LIST_ROWS]
+
+
+def interleave(copy, grouped, planes):
+    copy(
+        out=grouped.rearrange("p (c i) j -> p c j i", i=4),
+        in_=planes.rearrange("p j (c i) -> p c j i", i=4),
+    )
+
+
+def tile_picked_segunpool_none_p_kernel(
+    tc, x_words, x_scales, w1, w2, w3, offs, where, skip, out
+):
+    nc = tc.nc
+    with ExitStack() as ctx:
+        lists = ctx.enter_context(tc.tile_pool(name="lists", bufs=1))
+        keep = ctx.enter_context(tc.tile_pool(name="keep", bufs=1))
+        psum = ctx.enter_context(tc.psum_pool(name="psum", bufs=8))
+
+        def sbuf(shape, dtype, name, tag=None):
+            return keep.tile(shape, dtype, name=name, tag=tag or name, align_bytes=ALIGN)
+
+        def quantize(codes, scales, grouped):
+            nc.vector.quantize_mx(out=codes.bitcast(FP8X4), scales=scales, in_=grouped.rearrange("p c j -> p (c j)"))
+
+        def product(bank, w_codes, w_scales, tile, codes, scales, start, stop):
+            cols = slice(tile * P, (tile + 1) * P)
+            nc.tensor.matmul_mx(
+                out=bank,
+                lhsT=w_codes[:, cols].bitcast(FP8X4),
+                lhsT_scale=w_scales[:, cols],
+                rhs=codes.bitcast(FP8X4),
+                rhs_scale=scales,
+                start=start,
+                stop=stop,
+            )
+
+
+        scale_table = sbuf([P, T], U8, "scale_table")
+        nc.vector.memset(scale_table[:].bitcast(I32), 0)
+        for q in range(4):
+            nc.scalar.dma_start(
+                out=scale_table[32 * q : 32 * q + 4, :].bitcast(I32),
+                in_=x_scales[0, 4 * q : 4 * q + 4, :].bitcast(I32),
+            )
+        offs_t = lists.tile([P, S // LIST_ROWS], U16, name="offs_t")
+        nc.sync.dma_start(offs_t[:], offs)
+        skip_t = lists.tile([P, U // LIST_ROWS], U16, name="skip_t")
+        nc.sync.dma_start(skip_t[:], skip)
+
+        stage_tags = ("stage_a", "stage_b")
+        w1_rows = w1.rearrange("(p j) c -> p j c", j=PACK)
+        w1_raw = []
+        for h in range(2):
+            raw = sbuf([P, PACK, H // 2], F32, "w1_raw%d" % h, tag=stage_tags[h])
+            nc.sync.dma_start(out=raw[:], in_=w1_rows[:, :, h * (H // 2) : (h + 1) * (H // 2)])
+            w1_raw.append(raw)
+        word_table = sbuf([P, T], U32, "word_table")
+        nc.sync.dma_start(
+            out=word_table[:].bitcast(I32), in_=x_words[0].rearrange("p c r -> p (c r)").bitcast(I32)
+        )
+        where_t = lists.tile([P, S // LIST_ROWS], U16, name="where_t")
+        nc.sync.dma_start(where_t[:], where)
+
+        planes = sbuf([P, PACK * U], F32, "planes")
+        windows = {0: planes}
+        for t in (1, 2, 3):
+            windows[t] = sbuf([P, U], F32, "window%d" % t)
+            nc.vector.memset(windows[t][:], 0.0)
+        nc.vector.memset(planes[:, 0:U], 0.0)
+
+        picked_scales = sbuf([P, S], U8, "picked_scales")
+        nc.vector.tensor_copy(picked_scales[:], scale_table[:].indirect(offs_t[:]))
+        skip_scales = sbuf([P, U], U8, "skip_scales")
+        nc.vector.tensor_copy(skip_scales[:], scale_table[:].indirect(skip_t[:]))
+
+        w1_grouped = sbuf([P, H, PACK], BF16, "w1_grouped")
+        w1_dealt = w1_grouped[:].rearrange("p (t m) j -> p m j t", t=PACK)
+        for h in range(2):
+            nc.scalar.copy(
+                out=w1_dealt[:, h * (P // 2) : (h + 1) * (P // 2)],
+                in_=w1_raw[h][:].rearrange("p j (m t) -> p m j t", t=PACK),
+            )
+        w1_codes = sbuf([P, H], U32, "w1_codes")
+        w1_scales = sbuf([P, H], U8, "w1_scales")
+        quantize(w1_codes[:], w1_scales[:], w1_grouped[:])
+
+        w3_raw = sbuf([P, PACK, N], F32, "w3_raw", tag="stage_a")
+        nc.sync.dma_start(out=w3_raw[:], in_=w3.rearrange("(p j) c -> p j c", j=PACK))
+        w2_raw = sbuf([P, PACK, N], F32, "w2_raw", tag="stage_b")
+        nc.sync.dma_start(out=w2_raw[:], in_=w2.rearrange("(p j) c -> p j c", j=PACK))
+
+        picked_words = sbuf([P, S], U32, "picked_words")
+        for h in range(2):
+            nc.vector.tensor_copy(
+                picked_words[:, h * HALF : (h + 1) * HALF], word_table[:].indirect(entries(offs_t, h * HALF, HALF))
+            )
+
+        def project(t, h, tag=None):
+            bank = psum.tile([P, 512], F32, name="bank")
+            product(bank[:, 0:HALF], w1_codes, w1_scales, t, picked_words[:, h * HALF : (h + 1) * HALF],
+                    picked_scales[:, h * HALF : (h + 1) * HALF], True, True)
+            y = sbuf([P, HALF], F32, "y%d_%d" % (t, h), tag=tag)
+            nc.scalar.copy(out=y[:], in_=bank[:, 0:HALF])
+            return y
+
+        def project_whole(t, tag=None):
+            bank = psum.tile([P, 512], F32, name="bank")
+            product(bank[:], w1_codes, w1_scales, t, picked_words[:], picked_scales[:], True, True)
+            y = sbuf([P, S], F32, "y%d" % t, tag=tag)
+            nc.scalar.copy(out=y[:], in_=bank[:])
+            return y
+
+        def scatter(t, y, first, count):
+            nc.vector.tensor_copy(windows[t][:].indirect(entries(where_t, first, count)), y[:])
+
+        def gather_skip(words, c):
+            nc.vector.tensor_copy(words, word_table[:].indirect(entries(skip_t, c * CHUNK, CHUNK)))
+
+        y1a = project(1, 0)
+        y2 = project_whole(2)
+        y1b = project(1, 1)
+        scatter(1, y1a, 0, HALF)
+        scatter(2, y2, 0, S)
+        scatter(1, y1b, HALF, HALF)
+        skip_words = {}
+        skip_words[0] = sbuf([P, CHUNK], U32, "skip_words0")[:]
+        gather_skip(skip_words[0], 0)
+        for t in (1, 2):
+            nc.sync.dma_start(out=planes[:, t * U : (t + 1) * U], in_=windows[t][:])
+
+        w3_grouped = sbuf([P, N, PACK], BF16, "w3_grouped")
+        interleave(nc.scalar.copy, w3_grouped[:], w3_raw[:])
+        y3 = project_whole(3, tag="stage_a")
+        w2_grouped = sbuf([P, N, PACK], BF16, "w2_grouped")
+        interleave(nc.scalar.copy, w2_grouped[:], w2_raw[:])
+        y0a = project(0, 0)
+        y0b = project(0, 1)
+
+        scatter(3, y3, 0, S)
+        nc.scalar.copy(out=planes[:, 3 * U : 4 * U], in_=windows[3][:])
+        w2_codes = sbuf([P, N], U32, "w2_codes", tag="stage_a")
+        w2_scales = sbuf([P, N], U8, "w2_scales")
+        quantize(w2_codes[:], w2_scales[:], w2_grouped[:])
+        skip_words[1] = sbuf([P, CHUNK], U32, "skip_words1", tag="w2_grouped")[:]
+        gather_skip(skip_words[1], 1)
+
+        scatter(0, y0a, 0, HALF)
+        w3_codes = sbuf([P, N], U32, "w3_codes", tag="y0_0")
+        w3_scales = sbuf([P, N], U8, "w3_scales")
+        quantize(w3_codes[:], w3_scales[:], w3_grouped[:])
+        scatter(0, y0b, HALF, HALF)
+        late_words = sbuf([P, 2 * CHUNK], U32, "late_words", tag="y0_1")
+        skip_words[2] = late_words[:, 0:CHUNK]
+        skip_words[3] = late_words[:, CHUNK : 2 * CHUNK]
+
+        z_planes = planes[:].rearrange("p (t w) -> p t w", t=PACK)
+        out_tiles = out.rearrange("(m p) w -> p m w", p=P)
+        chunks = U // CHUNK
+        banks = {}
+
+        def open_groups(c):
+            cols = slice(c * CHUNK, (c + 1) * CHUNK)
+            banks[c] = []
+            for m in range(N // P):
+                bank = psum.tile([P, 512], F32, name="bank")
+                product(bank[:, 0:CHUNK], w3_codes, w3_scales, m, skip_words[c], skip_scales[:, cols], True, False)
+                banks[c].append(bank)
+
+        open_groups(0)
+        open_groups(1)
+        vector_cols = (VECTOR_SHARE, 0, CHUNK, CHUNK)
+        for c in range(chunks):
+            c0 = c * CHUNK
+            cols = slice(c0, c0 + CHUNK)
+            grouped = sbuf([P, CHUNK, PACK], BF16, "z_grouped%d" % c)
+            split = vector_cols[c]
+            if split > 0:
+                interleave(nc.vector.tensor_copy, grouped[:, 0:split, :], z_planes[:, :, c0 : c0 + split])
+            if split < CHUNK:
+                interleave(nc.scalar.copy, grouped[:, split:CHUNK, :], z_planes[:, :, c0 + split : c0 + CHUNK])
+            z_codes = sbuf([P, CHUNK], U32, "z_codes%d" % c)
+            z_scales = sbuf([P, CHUNK], U8, "z_scales%d" % c)
+            quantize(z_codes[:], z_scales[:], grouped[:])
+            if c >= 2:
+                open_groups(c)
+            for pair in range(2):
+                result = sbuf([P, 2, CHUNK], F32, "result%d_%d" % (c, pair))
+                for i in range(2):
+                    m = 2 * pair + i
+                    product(banks[c][m][:, 0:CHUNK], w2_codes, w2_scales, m, z_codes[:], z_scales[:], False, True)
+                    if c >= 2 and pair == 1:
+                        nc.vector.tensor_copy(out=result[:, i, :], in_=banks[c][m][:, 0:CHUNK])
+                    else:
+                        nc.scalar.copy(out=result[:, i, :], in_=banks[c][m][:, 0:CHUNK])
+                nc.sync.dma_start(out=out_tiles[:, 2 * pair : 2 * pair + 2, cols], in_=result[:])
+            if c + 2 < chunks:
+                gather_skip(skip_words[c + 2], c + 2)

@@ -28,8 +28,8 @@ def entries(lst, first, count):
 
 def interleave(copy, grouped, planes):
     copy(
-        out=grouped.rearrange("p (c i) j -> p c j i", i=4),
-        in_=planes.rearrange("p j (c i) -> p c j i", i=4),
+        out=grouped.rearrange("p (c i) j -> p c j i", i=2),
+        in_=planes.rearrange("p j (c i) -> p c j i", i=2),
     )
 
 
@@ -63,23 +63,20 @@ def tile_picked_segunpool_none_p_kernel(
 
         scale_table = sbuf([P, T], U8, "scale_table")
         nc.vector.memset(scale_table[:].bitcast(I32), 0)
-        for q in range(4):
-            nc.scalar.dma_start(
-                out=scale_table[32 * q : 32 * q + 4, :].bitcast(I32),
-                in_=x_scales[0, 4 * q : 4 * q + 4, :].bitcast(I32),
-            )
         offs_t = lists.tile([P, S // LIST_ROWS], U16, name="offs_t")
         nc.sync.dma_start(offs_t[:], offs)
         skip_t = lists.tile([P, U // LIST_ROWS], U16, name="skip_t")
         nc.sync.dma_start(skip_t[:], skip)
+        for q in range(4):
+            nc.sync.dma_start(
+                out=scale_table[32 * q : 32 * q + 4, :].bitcast(I32),
+                in_=x_scales[0, 4 * q : 4 * q + 4, :].bitcast(I32),
+            )
 
-        stage_tags = ("stage_a", "stage_b")
+        w1_raw = sbuf([P, PACK, H], F32, "w1_raw")
         w1_rows = w1.rearrange("(p j) c -> p j c", j=PACK)
-        w1_raw = []
-        for h in range(2):
-            raw = sbuf([P, PACK, H // 2], F32, "w1_raw%d" % h, tag=stage_tags[h])
-            nc.sync.dma_start(out=raw[:], in_=w1_rows[:, :, h * (H // 2) : (h + 1) * (H // 2)])
-            w1_raw.append(raw)
+        nc.scalar.dma_start(out=w1_raw[:, 0:2, :], in_=w1_rows[:, 0:2, :])
+        nc.sync.dma_start(out=w1_raw[:, 2:4, :], in_=w1_rows[:, 2:4, :])
         word_table = sbuf([P, T], U32, "word_table")
         nc.sync.dma_start(
             out=word_table[:].bitcast(I32), in_=x_words[0].rearrange("p c r -> p (c r)").bitcast(I32)
@@ -87,32 +84,36 @@ def tile_picked_segunpool_none_p_kernel(
         where_t = lists.tile([P, S // LIST_ROWS], U16, name="where_t")
         nc.sync.dma_start(where_t[:], where)
 
-        planes = sbuf([P, PACK * U], F32, "planes")
-        windows = {0: planes}
+        windows = {}
         for t in (1, 2, 3):
             windows[t] = sbuf([P, U], F32, "window%d" % t)
+        zero = sbuf([P, 8], F32, "zero")
+        nc.vector.memset(zero[:], 0.0)
+        for t in (1, 2):
             nc.vector.memset(windows[t][:], 0.0)
-        nc.vector.memset(planes[:, 0:U], 0.0)
+        nc.scalar.copy(out=windows[3][:], in_=zero[:, 0:1].to_broadcast([P, U]))
 
         picked_scales = sbuf([P, S], U8, "picked_scales")
         nc.vector.tensor_copy(picked_scales[:], scale_table[:].indirect(offs_t[:]))
-        skip_scales = sbuf([P, U], U8, "skip_scales")
-        nc.vector.tensor_copy(skip_scales[:], scale_table[:].indirect(skip_t[:]))
+        early_scales = sbuf([P, 3 * CHUNK], U8, "early_scales")
+        nc.vector.tensor_copy(early_scales[:], scale_table[:].indirect(entries(skip_t, 0, 3 * CHUNK)))
+        skip_scales = {c: early_scales[:, c * CHUNK : (c + 1) * CHUNK] for c in range(3)}
 
         w1_grouped = sbuf([P, H, PACK], BF16, "w1_grouped")
         w1_dealt = w1_grouped[:].rearrange("p (t m) j -> p m j t", t=PACK)
-        for h in range(2):
-            nc.scalar.copy(
-                out=w1_dealt[:, h * (P // 2) : (h + 1) * (P // 2)],
-                in_=w1_raw[h][:].rearrange("p j (m t) -> p m j t", t=PACK),
-            )
         w1_codes = sbuf([P, H], U32, "w1_codes")
         w1_scales = sbuf([P, H], U8, "w1_scales")
-        quantize(w1_codes[:], w1_scales[:], w1_grouped[:])
+        for u in range(2):
+            nc.scalar.copy(
+                out=w1_dealt[:, :, :, 2 * u : 2 * u + 2],
+                in_=w1_raw[:].rearrange("p j (m t) -> p m j t", t=PACK)[:, :, :, 2 * u : 2 * u + 2],
+            )
+        first, second = slice(0, H // 2), slice(H // 2, H)
+        quantize(w1_codes[:, first], w1_scales[:, first], w1_grouped[:, first, :])
 
         w3_raw = sbuf([P, PACK, N], F32, "w3_raw", tag="stage_a")
         nc.sync.dma_start(out=w3_raw[:], in_=w3.rearrange("(p j) c -> p j c", j=PACK))
-        w2_raw = sbuf([P, PACK, N], F32, "w2_raw", tag="stage_b")
+        w2_raw = sbuf([P, PACK, N], F32, "w2_raw")
         nc.sync.dma_start(out=w2_raw[:], in_=w2.rearrange("(p j) c -> p j c", j=PACK))
 
         picked_words = sbuf([P, S], U32, "picked_words")
@@ -120,6 +121,7 @@ def tile_picked_segunpool_none_p_kernel(
             nc.vector.tensor_copy(
                 picked_words[:, h * HALF : (h + 1) * HALF], word_table[:].indirect(entries(offs_t, h * HALF, HALF))
             )
+        quantize(w1_codes[:, second], w1_scales[:, second], w1_grouped[:, second, :])
 
         def project(t, h, tag=None):
             bank = psum.tile([P, 512], F32, name="bank")
@@ -145,6 +147,9 @@ def tile_picked_segunpool_none_p_kernel(
         y1a = project(1, 0)
         y2 = project_whole(2)
         y1b = project(1, 1)
+        planes = sbuf([P, PACK * U], F32, "planes", tag="w1_grouped")
+        windows[0] = planes
+        nc.scalar.copy(out=planes[:, 0:U], in_=zero[:, 0:1].to_broadcast([P, U]))
         scatter(1, y1a, 0, HALF)
         scatter(2, y2, 0, S)
         scatter(1, y1b, HALF, HALF)
@@ -175,9 +180,6 @@ def tile_picked_segunpool_none_p_kernel(
         w3_scales = sbuf([P, N], U8, "w3_scales")
         quantize(w3_codes[:], w3_scales[:], w3_grouped[:])
         scatter(0, y0b, HALF, HALF)
-        late_words = sbuf([P, 2 * CHUNK], U32, "late_words", tag="y0_1")
-        skip_words[2] = late_words[:, 0:CHUNK]
-        skip_words[3] = late_words[:, CHUNK : 2 * CHUNK]
 
         z_planes = planes[:].rearrange("p (t w) -> p t w", t=PACK)
         out_tiles = out.rearrange("(m p) w -> p m w", p=P)
@@ -189,35 +191,38 @@ def tile_picked_segunpool_none_p_kernel(
             banks[c] = []
             for m in range(N // P):
                 bank = psum.tile([P, 512], F32, name="bank")
-                product(bank[:, 0:CHUNK], w3_codes, w3_scales, m, skip_words[c], skip_scales[:, cols], True, False)
+                product(bank[:, 0:CHUNK], w3_codes, w3_scales, m, skip_words[c], skip_scales[c], True, False)
                 banks[c].append(bank)
 
         open_groups(0)
         open_groups(1)
-        vector_cols = (VECTOR_SHARE, 0, CHUNK, CHUNK)
         for c in range(chunks):
             c0 = c * CHUNK
             cols = slice(c0, c0 + CHUNK)
-            grouped = sbuf([P, CHUNK, PACK], BF16, "z_grouped%d" % c)
-            split = vector_cols[c]
-            if split > 0:
-                interleave(nc.vector.tensor_copy, grouped[:, 0:split, :], z_planes[:, :, c0 : c0 + split])
-            if split < CHUNK:
-                interleave(nc.scalar.copy, grouped[:, split:CHUNK, :], z_planes[:, :, c0 + split : c0 + CHUNK])
+            grouped = sbuf([P, CHUNK, PACK], BF16, "z_grouped%d" % c, tag="z_grouped%d" % min(c, 1))
+            interleave(nc.scalar.copy if c == 1 else nc.vector.tensor_copy, grouped[:], z_planes[:, :, cols])
+            if c == 2:
+                skip_words[3] = sbuf([P, CHUNK], U32, "skip_words3", tag="z_codes0")[:]
+                gather_skip(skip_words[3], 3)
+            if c == 3:
+                skip_scales[3] = sbuf([P, CHUNK], U8, "late_scales", tag="z_codes1")[:]
+                nc.vector.tensor_copy(skip_scales[3], scale_table[:].indirect(entries(skip_t, c0, CHUNK)))
             z_codes = sbuf([P, CHUNK], U32, "z_codes%d" % c)
             z_scales = sbuf([P, CHUNK], U8, "z_scales%d" % c)
             quantize(z_codes[:], z_scales[:], grouped[:])
+            if c == 0:
+                skip_words[2] = sbuf([P, CHUNK], U32, "skip_words2", tag="z_grouped0")[:]
+                gather_skip(skip_words[2], 2)
             if c >= 2:
                 open_groups(c)
-            for pair in range(2):
-                result = sbuf([P, 2, CHUNK], F32, "result%d_%d" % (c, pair))
-                for i in range(2):
-                    m = 2 * pair + i
+            per_store = 1 if c in (0, chunks - 1) else 2
+            for m0 in range(0, N // P, per_store):
+                result = sbuf([P, per_store, CHUNK], F32, "result%d_%d" % (c, m0))
+                for i in range(per_store):
+                    m = m0 + i
                     product(banks[c][m][:, 0:CHUNK], w2_codes, w2_scales, m, z_codes[:], z_scales[:], False, True)
-                    if c >= 2 and pair == 1:
+                    if c == chunks - 1 and m % 2 == 1:
                         nc.vector.tensor_copy(out=result[:, i, :], in_=banks[c][m][:, 0:CHUNK])
                     else:
                         nc.scalar.copy(out=result[:, i, :], in_=banks[c][m][:, 0:CHUNK])
-                nc.sync.dma_start(out=out_tiles[:, 2 * pair : 2 * pair + 2, cols], in_=result[:])
-            if c + 2 < chunks:
-                gather_skip(skip_words[c + 2], c + 2)
+                nc.sync.dma_start(out=out_tiles[:, m0 : m0 + per_store, cols], in_=result[:])

@@ -84,13 +84,14 @@ def tile_picked_segunpool_none_p_kernel(
         where_t = lists.tile([P, S // LIST_ROWS], U16, name="where_t")
         nc.sync.dma_start(where_t[:], where)
 
-        windows = {}
+        planes = sbuf([P, PACK * U], F32, "planes")
+        windows = {0: planes}
         for t in (1, 2, 3):
             windows[t] = sbuf([P, U], F32, "window%d" % t)
         zero = sbuf([P, 8], F32, "zero")
         nc.vector.memset(zero[:], 0.0)
-        for t in (1, 2):
-            nc.vector.memset(windows[t][:], 0.0)
+        for t in (1, 2, 0):
+            nc.vector.memset(windows[t][:, 0:U], 0.0)
         nc.scalar.copy(out=windows[3][:], in_=zero[:, 0:1].to_broadcast([P, U]))
 
         picked_scales = sbuf([P, S], U8, "picked_scales")
@@ -147,9 +148,6 @@ def tile_picked_segunpool_none_p_kernel(
         y1a = project(1, 0)
         y2 = project_whole(2)
         y1b = project(1, 1)
-        planes = sbuf([P, PACK * U], F32, "planes", tag="w1_grouped")
-        windows[0] = planes
-        nc.scalar.copy(out=planes[:, 0:U], in_=zero[:, 0:1].to_broadcast([P, U]))
         scatter(1, y1a, 0, HALF)
         scatter(2, y2, 0, S)
         scatter(1, y1b, HALF, HALF)

@@ -15,21 +15,27 @@ FP8X4 = mybir.dt.float8_e4m3fn_x4
 
 P = 128
 PACK = 4
+QUADRANTS = 4
 LIST_ROWS = 16
+ALIGN = 64
+BANKS = 8
+BANK_COLS = 512
 HALF = S // 2
 CHUNK = 256
-ALIGN = 64
-VECTOR_SHARE = 160
+CHUNKS = U // CHUNK
+M_TILES = N // P
+VECTOR_COLS = (CHUNK, 0, CHUNK // 4, CHUNK)
+VECTOR_BANKS = ((2, 2), (2, 3), (3, 1), (3, 3))
 
 
-def entries(lst, first, count):
-    return lst[:, first // LIST_ROWS : (first + count) // LIST_ROWS]
+def entries(list_tile, first, count):
+    return list_tile[:, first // LIST_ROWS : (first + count) // LIST_ROWS]
 
 
-def interleave(copy, grouped, planes):
+def interleave(copy, grouped, rows):
     copy(
         out=grouped.rearrange("p (c i) j -> p c j i", i=2),
-        in_=planes.rearrange("p j (c i) -> p c j i", i=2),
+        in_=rows.rearrange("p j (c i) -> p c j i", i=2),
     )
 
 
@@ -40,26 +46,25 @@ def tile_picked_segunpool_none_p_kernel(
     with ExitStack() as ctx:
         lists = ctx.enter_context(tc.tile_pool(name="lists", bufs=1))
         keep = ctx.enter_context(tc.tile_pool(name="keep", bufs=1))
-        psum = ctx.enter_context(tc.psum_pool(name="psum", bufs=8))
+        psum = ctx.enter_context(tc.psum_pool(name="psum", bufs=BANKS))
 
-        def sbuf(shape, dtype, name, tag=None):
-            return keep.tile(shape, dtype, name=name, tag=tag or name, align_bytes=ALIGN)
+        def sbuf(shape, dtype, name, after=None):
+            return keep.tile(shape, dtype, name=name, tag=after or name, align_bytes=ALIGN)
 
         def quantize(codes, scales, grouped):
             nc.vector.quantize_mx(out=codes.bitcast(FP8X4), scales=scales, in_=grouped.rearrange("p c j -> p (c j)"))
 
-        def product(bank, w_codes, w_scales, tile, codes, scales, start, stop):
-            cols = slice(tile * P, (tile + 1) * P)
+        def product(acc, w_codes, w_scales, w_tile, codes, scales, start, stop):
+            w_cols = slice(w_tile * P, (w_tile + 1) * P)
             nc.tensor.matmul_mx(
-                out=bank,
-                lhsT=w_codes[:, cols].bitcast(FP8X4),
-                lhsT_scale=w_scales[:, cols],
+                out=acc,
+                lhsT=w_codes[:, w_cols].bitcast(FP8X4),
+                lhsT_scale=w_scales[:, w_cols],
                 rhs=codes.bitcast(FP8X4),
                 rhs_scale=scales,
                 start=start,
                 stop=stop,
             )
-
 
         scale_table = sbuf([P, T], U8, "scale_table")
         nc.vector.memset(scale_table[:].bitcast(I32), 0)
@@ -67,7 +72,7 @@ def tile_picked_segunpool_none_p_kernel(
         nc.sync.dma_start(offs_t[:], offs)
         skip_t = lists.tile([P, U // LIST_ROWS], U16, name="skip_t")
         nc.sync.dma_start(skip_t[:], skip)
-        for q in range(4):
+        for q in range(QUADRANTS):
             nc.sync.dma_start(
                 out=scale_table[32 * q : 32 * q + 4, :].bitcast(I32),
                 in_=x_scales[0, 4 * q : 4 * q + 4, :].bitcast(I32),
@@ -88,139 +93,131 @@ def tile_picked_segunpool_none_p_kernel(
         windows = {0: planes}
         for t in (1, 2, 3):
             windows[t] = sbuf([P, U], F32, "window%d" % t)
-        zero = sbuf([P, 8], F32, "zero")
+        zero = sbuf([P, 1], F32, "zero")
         nc.vector.memset(zero[:], 0.0)
-        for t in (1, 2, 0):
-            nc.vector.memset(windows[t][:, 0:U], 0.0)
-        nc.scalar.copy(out=windows[3][:], in_=zero[:, 0:1].to_broadcast([P, U]))
+        for t in (1, 2):
+            nc.vector.memset(windows[t][:], 0.0)
+        for t in (3, 0):
+            nc.scalar.copy(out=windows[t][:, 0:U], in_=zero[:].to_broadcast([P, U]))
 
         picked_scales = sbuf([P, S], U8, "picked_scales")
         nc.vector.tensor_copy(picked_scales[:], scale_table[:].indirect(offs_t[:]))
-        early_scales = sbuf([P, 3 * CHUNK], U8, "early_scales")
-        nc.vector.tensor_copy(early_scales[:], scale_table[:].indirect(entries(skip_t, 0, 3 * CHUNK)))
-        skip_scales = {c: early_scales[:, c * CHUNK : (c + 1) * CHUNK] for c in range(3)}
+        skip_scales = sbuf([P, U], U8, "skip_scales")
+        nc.vector.tensor_copy(skip_scales[:], scale_table[:].indirect(skip_t[:]))
 
         w1_grouped = sbuf([P, H, PACK], BF16, "w1_grouped")
         w1_dealt = w1_grouped[:].rearrange("p (t m) j -> p m j t", t=PACK)
         w1_codes = sbuf([P, H], U32, "w1_codes")
         w1_scales = sbuf([P, H], U8, "w1_scales")
-        for u in range(2):
+        for pair in (slice(0, 2), slice(2, 4)):
             nc.scalar.copy(
-                out=w1_dealt[:, :, :, 2 * u : 2 * u + 2],
-                in_=w1_raw[:].rearrange("p j (m t) -> p m j t", t=PACK)[:, :, :, 2 * u : 2 * u + 2],
+                out=w1_dealt[:, :, :, pair],
+                in_=w1_raw[:].rearrange("p j (m t) -> p m j t", t=PACK)[:, :, :, pair],
             )
-        first, second = slice(0, H // 2), slice(H // 2, H)
-        quantize(w1_codes[:, first], w1_scales[:, first], w1_grouped[:, first, :])
+        first_pair, second_pair = slice(0, H // 2), slice(H // 2, H)
+        quantize(w1_codes[:, first_pair], w1_scales[:, first_pair], w1_grouped[:, first_pair, :])
 
-        w3_raw = sbuf([P, PACK, N], F32, "w3_raw", tag="stage_a")
+        w3_raw = sbuf([P, PACK, N], F32, "w3_raw")
         nc.sync.dma_start(out=w3_raw[:], in_=w3.rearrange("(p j) c -> p j c", j=PACK))
         w2_raw = sbuf([P, PACK, N], F32, "w2_raw")
         nc.sync.dma_start(out=w2_raw[:], in_=w2.rearrange("(p j) c -> p j c", j=PACK))
 
         picked_words = sbuf([P, S], U32, "picked_words")
-        for h in range(2):
+        for first in (0, HALF):
             nc.vector.tensor_copy(
-                picked_words[:, h * HALF : (h + 1) * HALF], word_table[:].indirect(entries(offs_t, h * HALF, HALF))
+                picked_words[:, first : first + HALF], word_table[:].indirect(entries(offs_t, first, HALF))
             )
-        quantize(w1_codes[:, second], w1_scales[:, second], w1_grouped[:, second, :])
+        quantize(w1_codes[:, second_pair], w1_scales[:, second_pair], w1_grouped[:, second_pair, :])
 
-        def project(t, h, tag=None):
-            bank = psum.tile([P, 512], F32, name="bank")
-            product(bank[:, 0:HALF], w1_codes, w1_scales, t, picked_words[:, h * HALF : (h + 1) * HALF],
-                    picked_scales[:, h * HALF : (h + 1) * HALF], True, True)
-            y = sbuf([P, HALF], F32, "y%d_%d" % (t, h), tag=tag)
-            nc.scalar.copy(out=y[:], in_=bank[:, 0:HALF])
-            return y
-
-        def project_whole(t, tag=None):
-            bank = psum.tile([P, 512], F32, name="bank")
-            product(bank[:], w1_codes, w1_scales, t, picked_words[:], picked_scales[:], True, True)
-            y = sbuf([P, S], F32, "y%d" % t, tag=tag)
-            nc.scalar.copy(out=y[:], in_=bank[:])
+        def project(t, first, count, after=None):
+            picked = slice(first, first + count)
+            bank = psum.tile([P, BANK_COLS], F32, name="bank")
+            product(bank[:, 0:count], w1_codes, w1_scales, t, picked_words[:, picked], picked_scales[:, picked], True, True)
+            y = sbuf([P, count], F32, "y%d_%d" % (t, first), after=after)
+            nc.scalar.copy(out=y[:], in_=bank[:, 0:count])
             return y
 
         def scatter(t, y, first, count):
             nc.vector.tensor_copy(windows[t][:].indirect(entries(where_t, first, count)), y[:])
 
-        def gather_skip(words, c):
-            nc.vector.tensor_copy(words, word_table[:].indirect(entries(skip_t, c * CHUNK, CHUNK)))
-
-        y1a = project(1, 0)
-        y2 = project_whole(2)
-        y1b = project(1, 1)
-        scatter(1, y1a, 0, HALF)
-        scatter(2, y2, 0, S)
-        scatter(1, y1b, HALF, HALF)
         skip_words = {}
-        skip_words[0] = sbuf([P, CHUNK], U32, "skip_words0")[:]
-        gather_skip(skip_words[0], 0)
+
+        def gather_skip(c, after=None):
+            skip_words[c] = sbuf([P, CHUNK], U32, "skip_words%d" % c, after=after)
+            nc.vector.tensor_copy(skip_words[c][:], word_table[:].indirect(entries(skip_t, c * CHUNK, CHUNK)))
+
+        y1_low = project(1, 0, HALF)
+        y2 = project(2, 0, S)
+        y1_high = project(1, HALF, HALF)
+        scatter(1, y1_low, 0, HALF)
+        scatter(2, y2, 0, S)
+        scatter(1, y1_high, HALF, HALF)
+        gather_skip(0)
         for t in (1, 2):
             nc.sync.dma_start(out=planes[:, t * U : (t + 1) * U], in_=windows[t][:])
 
         w3_grouped = sbuf([P, N, PACK], BF16, "w3_grouped")
         interleave(nc.scalar.copy, w3_grouped[:], w3_raw[:])
-        y3 = project_whole(3, tag="stage_a")
+        y3 = project(3, 0, S, after="w3_raw")
         w2_grouped = sbuf([P, N, PACK], BF16, "w2_grouped")
         interleave(nc.scalar.copy, w2_grouped[:], w2_raw[:])
-        y0a = project(0, 0)
-        y0b = project(0, 1)
+        y0_low = project(0, 0, HALF)
+        y0_high = project(0, HALF, HALF)
 
         scatter(3, y3, 0, S)
         nc.scalar.copy(out=planes[:, 3 * U : 4 * U], in_=windows[3][:])
-        w2_codes = sbuf([P, N], U32, "w2_codes", tag="stage_a")
+        w2_codes = sbuf([P, N], U32, "w2_codes", after="w3_raw")
         w2_scales = sbuf([P, N], U8, "w2_scales")
         quantize(w2_codes[:], w2_scales[:], w2_grouped[:])
-        skip_words[1] = sbuf([P, CHUNK], U32, "skip_words1", tag="w2_grouped")[:]
-        gather_skip(skip_words[1], 1)
+        gather_skip(1, after="w2_grouped")
 
-        scatter(0, y0a, 0, HALF)
-        w3_codes = sbuf([P, N], U32, "w3_codes", tag="y0_0")
+        scatter(0, y0_low, 0, HALF)
+        w3_codes = sbuf([P, N], U32, "w3_codes", after="y0_0")
         w3_scales = sbuf([P, N], U8, "w3_scales")
         quantize(w3_codes[:], w3_scales[:], w3_grouped[:])
-        scatter(0, y0b, HALF, HALF)
+        scatter(0, y0_high, HALF, HALF)
 
         z_planes = planes[:].rearrange("p (t w) -> p t w", t=PACK)
         out_tiles = out.rearrange("(m p) w -> p m w", p=P)
-        chunks = U // CHUNK
         banks = {}
 
         def open_groups(c):
-            cols = slice(c * CHUNK, (c + 1) * CHUNK)
             banks[c] = []
-            for m in range(N // P):
-                bank = psum.tile([P, 512], F32, name="bank")
-                product(bank[:, 0:CHUNK], w3_codes, w3_scales, m, skip_words[c], skip_scales[c], True, False)
+            for m in range(M_TILES):
+                bank = psum.tile([P, BANK_COLS], F32, name="bank")
+                product(
+                    bank[:, 0:CHUNK], w3_codes, w3_scales, m,
+                    skip_words[c][:], skip_scales[:, c * CHUNK : (c + 1) * CHUNK], True, False,
+                )
                 banks[c].append(bank)
 
         open_groups(0)
         open_groups(1)
-        for c in range(chunks):
+        for c in range(CHUNKS):
             c0 = c * CHUNK
-            cols = slice(c0, c0 + CHUNK)
-            grouped = sbuf([P, CHUNK, PACK], BF16, "z_grouped%d" % c, tag="z_grouped%d" % min(c, 1))
-            interleave(nc.scalar.copy if c == 1 else nc.vector.tensor_copy, grouped[:], z_planes[:, :, cols])
+            last = c == CHUNKS - 1
+            grouped = sbuf([P, CHUNK, PACK], BF16, "z_grouped%d" % c, after="z_grouped2" if last else None)
+            split = VECTOR_COLS[c]
+            if split > 0:
+                interleave(nc.vector.tensor_copy, grouped[:, 0:split, :], z_planes[:, :, c0 : c0 + split])
+            if split < CHUNK:
+                interleave(nc.scalar.copy, grouped[:, split:CHUNK, :], z_planes[:, :, c0 + split : c0 + CHUNK])
             if c == 2:
-                skip_words[3] = sbuf([P, CHUNK], U32, "skip_words3", tag="z_codes0")[:]
-                gather_skip(skip_words[3], 3)
-            if c == 3:
-                skip_scales[3] = sbuf([P, CHUNK], U8, "late_scales", tag="z_codes1")[:]
-                nc.vector.tensor_copy(skip_scales[3], scale_table[:].indirect(entries(skip_t, c0, CHUNK)))
+                gather_skip(3, after="z_grouped1")
             z_codes = sbuf([P, CHUNK], U32, "z_codes%d" % c)
             z_scales = sbuf([P, CHUNK], U8, "z_scales%d" % c)
             quantize(z_codes[:], z_scales[:], grouped[:])
             if c == 0:
-                skip_words[2] = sbuf([P, CHUNK], U32, "skip_words2", tag="z_grouped0")[:]
-                gather_skip(skip_words[2], 2)
+                gather_skip(2, after="z_grouped0")
             if c >= 2:
                 open_groups(c)
-            per_store = 1 if c in (0, chunks - 1) else 2
-            for m0 in range(0, N // P, per_store):
+            per_store = 1 if c == 0 or last else 2
+            for m0 in range(0, M_TILES, per_store):
                 result = sbuf([P, per_store, CHUNK], F32, "result%d_%d" % (c, m0))
                 for i in range(per_store):
                     m = m0 + i
-                    product(banks[c][m][:, 0:CHUNK], w2_codes, w2_scales, m, z_codes[:], z_scales[:], False, True)
-                    if c == chunks - 1 and m % 2 == 1:
-                        nc.vector.tensor_copy(out=result[:, i, :], in_=banks[c][m][:, 0:CHUNK])
-                    else:
-                        nc.scalar.copy(out=result[:, i, :], in_=banks[c][m][:, 0:CHUNK])
-                nc.sync.dma_start(out=out_tiles[:, m0 : m0 + per_store, cols], in_=result[:])
+                    acc = banks[c][m][:, 0:CHUNK]
+                    product(acc, w2_codes, w2_scales, m, z_codes[:], z_scales[:], False, True)
+                    copy = nc.vector.tensor_copy if (c, m) in VECTOR_BANKS else nc.scalar.copy
+                    copy(out=result[:, i, :], in_=acc)
+                nc.sync.dma_start(out=out_tiles[:, m0 : m0 + per_store, c0 : c0 + CHUNK], in_=result[:])

@@ -21,11 +21,12 @@ ALIGN = 64
 BANKS = 8
 BANK_COLS = 512
 HALF = S // 2
-CHUNK = 256
-CHUNKS = U // CHUNK
 M_TILES = N // P
-VECTOR_COLS = (CHUNK, 0, CHUNK // 4, CHUNK)
-VECTOR_BANKS = ((2, 2), (2, 3), (3, 1), (3, 3))
+CHUNK = 256
+CHUNKS = tuple((c0, CHUNK) for c0 in range(0, U, CHUNK))
+LATE = U - CHUNK
+CHUNK_BANKS = {0: (0, 1, 2, 3), 256: (4, 5), 512: (6, 7), 768: (0, 1, 2, 3)}
+VECTOR_BANKS = ((256, 4), (768, 0), (768, 2))
 
 
 def entries(list_tile, first, count):
@@ -46,10 +47,13 @@ def tile_picked_segunpool_none_p_kernel(
     with ExitStack() as ctx:
         lists = ctx.enter_context(tc.tile_pool(name="lists", bufs=1))
         keep = ctx.enter_context(tc.tile_pool(name="keep", bufs=1))
-        psum = ctx.enter_context(tc.psum_pool(name="psum", bufs=BANKS))
+        psum = ctx.enter_context(tc.psum_pool(name="psum", bufs=1))
 
         def sbuf(shape, dtype, name, after=None):
             return keep.tile(shape, dtype, name=name, tag=after or name, align_bytes=ALIGN)
+
+        def bank_tile(b, name):
+            return psum.tile([P, BANK_COLS], F32, name=name, tag="bank%d" % b)
 
         def quantize(codes, scales, grouped):
             nc.vector.quantize_mx(out=codes.bitcast(FP8X4), scales=scales, in_=grouped.rearrange("p c j -> p (c j)"))
@@ -68,156 +72,173 @@ def tile_picked_segunpool_none_p_kernel(
 
         scale_table = sbuf([P, T], U8, "scale_table")
         nc.vector.memset(scale_table[:].bitcast(I32), 0)
+        w1_raw = sbuf([P, PACK, H], F32, "w1_raw")
+        w1_rows = w1.rearrange("(p j) c -> p j c", j=PACK)
+        nc.scalar.dma_start(out=w1_raw[:, 0:2, :], in_=w1_rows[:, 0:2, :])
         offs_t = lists.tile([P, S // LIST_ROWS], U16, name="offs_t")
         nc.sync.dma_start(offs_t[:], offs)
-        skip_t = lists.tile([P, U // LIST_ROWS], U16, name="skip_t")
-        nc.sync.dma_start(skip_t[:], skip)
         for q in range(QUADRANTS):
             nc.sync.dma_start(
                 out=scale_table[32 * q : 32 * q + 4, :].bitcast(I32),
                 in_=x_scales[0, 4 * q : 4 * q + 4, :].bitcast(I32),
             )
-
-        w1_raw = sbuf([P, PACK, H], F32, "w1_raw")
-        w1_rows = w1.rearrange("(p j) c -> p j c", j=PACK)
-        nc.scalar.dma_start(out=w1_raw[:, 0:2, :], in_=w1_rows[:, 0:2, :])
-        nc.sync.dma_start(out=w1_raw[:, 2:4, :], in_=w1_rows[:, 2:4, :])
+        skip_t = lists.tile([P, U // LIST_ROWS], U16, name="skip_t")
+        nc.sync.dma_start(skip_t[:], skip)
         word_table = sbuf([P, T], U32, "word_table")
         nc.sync.dma_start(
             out=word_table[:].bitcast(I32), in_=x_words[0].rearrange("p c r -> p (c r)").bitcast(I32)
         )
+        nc.sync.dma_start(out=w1_raw[:, 2:4, :], in_=w1_rows[:, 2:4, :])
         where_t = lists.tile([P, S // LIST_ROWS], U16, name="where_t")
         nc.sync.dma_start(where_t[:], where)
+        w3_raw = sbuf([P, PACK, N], F32, "w3_raw")
+        nc.sync.dma_start(out=w3_raw[:], in_=w3.rearrange("(p j) c -> p j c", j=PACK))
+        w2_raw = sbuf([P, PACK, N], F32, "w2_raw")
+        w2_rows = w2.rearrange("(b t q) c -> t b q c", t=PACK, q=8)
+        for t in range(PACK):
+            nc.sync.dma_start(out=w2_raw[:, t, :], in_=w2_rows[t])
 
-        planes = sbuf([P, PACK * U], F32, "planes")
-        windows = {0: planes}
-        for t in (1, 2, 3):
-            windows[t] = sbuf([P, U], F32, "window%d" % t)
+        pairs = {t: sbuf([P, 2 * U], F32, "pair%d" % t) for t in (0, 2)}
+        windows = {t: pairs[t] if t in pairs else sbuf([P, U], F32, "window%d" % t) for t in range(PACK)}
         zero = sbuf([P, 1], F32, "zero")
         nc.vector.memset(zero[:], 0.0)
-        for t in (1, 2):
+        for t in (3, 1):
             nc.vector.memset(windows[t][:], 0.0)
-        for t in (3, 0):
+        for t in (2, 0):
             nc.scalar.copy(out=windows[t][:, 0:U], in_=zero[:].to_broadcast([P, U]))
 
         picked_scales = sbuf([P, S], U8, "picked_scales")
         nc.vector.tensor_copy(picked_scales[:], scale_table[:].indirect(offs_t[:]))
-        skip_scales = sbuf([P, U], U8, "skip_scales")
-        nc.vector.tensor_copy(skip_scales[:], scale_table[:].indirect(skip_t[:]))
+        skip_scales, skip_words = {}, {}
 
-        w1_grouped = sbuf([P, H, PACK], BF16, "w1_grouped")
-        w1_dealt = w1_grouped[:].rearrange("p (t m) j -> p m j t", t=PACK)
-        w1_codes = sbuf([P, H], U32, "w1_codes")
-        w1_scales = sbuf([P, H], U8, "w1_scales")
-        for pair in (slice(0, 2), slice(2, 4)):
-            nc.scalar.copy(
-                out=w1_dealt[:, :, :, pair],
-                in_=w1_raw[:].rearrange("p j (m t) -> p m j t", t=PACK)[:, :, :, pair],
-            )
-        first_pair, second_pair = slice(0, H // 2), slice(H // 2, H)
-        quantize(w1_codes[:, first_pair], w1_scales[:, first_pair], w1_grouped[:, first_pair, :])
+        def gather_skip(store, table, dtype, first, count, after=None):
+            tile = sbuf([P, count], dtype, "skip%d_%d" % (store is skip_words, first), after=after)
+            nc.vector.tensor_copy(tile[:], table[:].indirect(entries(skip_t, first, count)))
+            for c0, cols in CHUNKS:
+                if first <= c0 < first + count:
+                    store[c0] = tile[:, c0 - first : c0 - first + cols]
 
-        w3_raw = sbuf([P, PACK, N], F32, "w3_raw")
-        nc.sync.dma_start(out=w3_raw[:], in_=w3.rearrange("(p j) c -> p j c", j=PACK))
-        w2_raw = sbuf([P, PACK, N], F32, "w2_raw")
-        nc.sync.dma_start(out=w2_raw[:], in_=w2.rearrange("(p j) c -> p j c", j=PACK))
+        gather_skip(skip_scales, scale_table, U8, 0, LATE)
 
         picked_words = sbuf([P, S], U32, "picked_words")
-        for first in (0, HALF):
-            nc.vector.tensor_copy(
-                picked_words[:, first : first + HALF], word_table[:].indirect(entries(offs_t, first, HALF))
-            )
-        quantize(w1_codes[:, second_pair], w1_scales[:, second_pair], w1_grouped[:, second_pair, :])
+        nc.vector.tensor_copy(picked_words[:], word_table[:].indirect(offs_t[:]))
 
-        def project(t, first, count, after=None):
+        w1_planes = w1_raw[:].rearrange("p j (b t h i) -> p t b h j i", t=PACK, h=2, i=4)
+        w1_codes, w1_scales = {}, {}
+
+        def quantize_w1(ts):
+            name = "%d" % ts[0]
+            grouped = sbuf([P, len(ts) * P, PACK], BF16, "w1_grouped" + name)
+            codes = sbuf([P, len(ts) * P], U32, "w1_codes" + name)
+            scales = sbuf([P, len(ts) * P], U8, "w1_scales" + name)
+            for n, t in enumerate(ts):
+                cols = slice(n * P, (n + 1) * P)
+                nc.scalar.copy(out=grouped[:, cols, :].rearrange("p (b h i) j -> p b h j i", h=2, i=4), in_=w1_planes[:, t])
+                w1_codes[t], w1_scales[t] = codes[:, cols], scales[:, cols]
+            quantize(codes[:], scales[:], grouped[:])
+
+        def project(t, first, count, b, after=None):
             picked = slice(first, first + count)
-            bank = psum.tile([P, BANK_COLS], F32, name="bank")
-            product(bank[:, 0:count], w1_codes, w1_scales, t, picked_words[:, picked], picked_scales[:, picked], True, True)
+            bank = bank_tile(b, "y_bank%d_%d" % (t, first))
+            product(bank[:, 0:count], w1_codes[t], w1_scales[t], 0, picked_words[:, picked], picked_scales[:, picked], True, True)
             y = sbuf([P, count], F32, "y%d_%d" % (t, first), after=after)
             nc.scalar.copy(out=y[:], in_=bank[:, 0:count])
-            return y
+            return y[:]
 
         def scatter(t, y, first, count):
-            nc.vector.tensor_copy(windows[t][:].indirect(entries(where_t, first, count)), y[:])
+            nc.vector.tensor_copy(windows[t][:].indirect(entries(where_t, first, count)), y)
 
-        skip_words = {}
+        def pair_rows(t):
+            return pairs[t][:].rearrange("p (t w) -> p t w", t=2)
 
-        def gather_skip(c, after=None):
-            skip_words[c] = sbuf([P, CHUNK], U32, "skip_words%d" % c, after=after)
-            nc.vector.tensor_copy(skip_words[c][:], word_table[:].indirect(entries(skip_t, c * CHUNK, CHUNK)))
-
-        y1_low = project(1, 0, HALF)
-        y2 = project(2, 0, S)
-        y1_high = project(1, HALF, HALF)
-        scatter(1, y1_low, 0, HALF)
-        scatter(2, y2, 0, S)
-        scatter(1, y1_high, HALF, HALF)
-        gather_skip(0)
-        for t in (1, 2):
-            nc.sync.dma_start(out=planes[:, t * U : (t + 1) * U], in_=windows[t][:])
-
-        w3_grouped = sbuf([P, N, PACK], BF16, "w3_grouped")
-        interleave(nc.scalar.copy, w3_grouped[:], w3_raw[:])
-        y3 = project(3, 0, S, after="w3_raw")
-        w2_grouped = sbuf([P, N, PACK], BF16, "w2_grouped")
-        interleave(nc.scalar.copy, w2_grouped[:], w2_raw[:])
-        y0_low = project(0, 0, HALF)
-        y0_high = project(0, HALF, HALF)
-
+        quantize_w1((3,))
+        y3 = project(3, 0, S, 7)
+        gather_skip(skip_words, word_table, U32, 0, LATE, after="w1_grouped3")
+        quantize_w1((1,))
         scatter(3, y3, 0, S)
-        nc.scalar.copy(out=planes[:, 3 * U : 4 * U], in_=windows[3][:])
-        w2_codes = sbuf([P, N], U32, "w2_codes", after="w3_raw")
-        w2_scales = sbuf([P, N], U8, "w2_scales")
+        nc.sync.dma_start(out=pairs[2][:, U : 2 * U], in_=windows[3][:])
+        quantize_w1((2, 0))
+        y1 = project(1, 0, S, 6, after="w1_raw")
+        scatter(1, y1, 0, S)
+        nc.sync.dma_start(out=pairs[0][:, U : 2 * U], in_=windows[1][:])
+        y2 = project(2, 0, S, 4)
+        y0 = project(0, 0, S, 3)
+
+        w3_grouped = sbuf([P, N, PACK], BF16, "w3_grouped", after="w1_codes1")
+        interleave(nc.scalar.copy, w3_grouped[:], w3_raw[:])
+        w2_grouped = sbuf([P, N, PACK], BF16, "w2_grouped", after="w1_codes2")
+        interleave(nc.scalar.copy, w2_grouped[:], w2_raw[:])
+
+        scatter(2, y2, 0, S)
+        grouped = {}
+        for c0, cols in CHUNKS:
+            grouped[c0] = sbuf([P, cols, PACK], BF16, "z_grouped%d" % c0)[:]
+            interleave(nc.scalar.copy, grouped[c0][:, :, 2:4], pair_rows(2)[:, :, c0 : c0 + cols])
+        w2_codes = sbuf([P, N], U32, "w2_codes")
+        w2_scales = sbuf([P, N], U8, "w2_scales", after="y1_0")
         quantize(w2_codes[:], w2_scales[:], w2_grouped[:])
-        gather_skip(1, after="w2_grouped")
-
-        scatter(0, y0_low, 0, HALF)
-        w3_codes = sbuf([P, N], U32, "w3_codes", after="y0_0")
-        w3_scales = sbuf([P, N], U8, "w3_scales")
+        w3_codes = sbuf([P, N], U32, "w3_codes")
+        w3_scales = sbuf([P, N], U8, "w3_scales", after="y2_0")
         quantize(w3_codes[:], w3_scales[:], w3_grouped[:])
-        scatter(0, y0_high, HALF, HALF)
+        scatter(0, y0, 0, S)
 
-        z_planes = planes[:].rearrange("p (t w) -> p t w", t=PACK)
         out_tiles = out.rearrange("(m p) w -> p m w", p=P)
         banks = {}
 
-        def open_groups(c):
-            banks[c] = []
-            for m in range(M_TILES):
-                bank = psum.tile([P, BANK_COLS], F32, name="bank")
+        def side_by_side(c0, cols, b, w_codes, w_scales, codes, scales, opens):
+            per_bank = M_TILES // len(CHUNK_BANKS[c0])
+            if opens:
+                banks[c0, b] = bank_tile(b, "out_bank%d_%d" % (c0, b))
+            for i in range(per_bank):
                 product(
-                    bank[:, 0:CHUNK], w3_codes, w3_scales, m,
-                    skip_words[c][:], skip_scales[:, c * CHUNK : (c + 1) * CHUNK], True, False,
+                    banks[c0, b][:, i * cols : (i + 1) * cols], w_codes, w_scales, CHUNK_BANKS[c0].index(b) * per_bank + i,
+                    codes, scales, opens and i == 0, not opens and i == per_bank - 1,
                 )
-                banks[c].append(bank)
 
-        open_groups(0)
-        open_groups(1)
-        for c in range(CHUNKS):
-            c0 = c * CHUNK
-            last = c == CHUNKS - 1
-            grouped = sbuf([P, CHUNK, PACK], BF16, "z_grouped%d" % c, after="z_grouped2" if last else None)
-            split = VECTOR_COLS[c]
-            if split > 0:
-                interleave(nc.vector.tensor_copy, grouped[:, 0:split, :], z_planes[:, :, c0 : c0 + split])
-            if split < CHUNK:
-                interleave(nc.scalar.copy, grouped[:, split:CHUNK, :], z_planes[:, :, c0 + split : c0 + CHUNK])
-            if c == 2:
-                gather_skip(3, after="z_grouped1")
-            z_codes = sbuf([P, CHUNK], U32, "z_codes%d" % c)
-            z_scales = sbuf([P, CHUNK], U8, "z_scales%d" % c)
-            quantize(z_codes[:], z_scales[:], grouped[:])
-            if c == 0:
-                gather_skip(2, after="z_grouped0")
-            if c >= 2:
-                open_groups(c)
-            per_store = 1 if c == 0 or last else 2
-            for m0 in range(0, M_TILES, per_store):
-                result = sbuf([P, per_store, CHUNK], F32, "result%d_%d" % (c, m0))
-                for i in range(per_store):
-                    m = m0 + i
-                    acc = banks[c][m][:, 0:CHUNK]
-                    product(acc, w2_codes, w2_scales, m, z_codes[:], z_scales[:], False, True)
-                    copy = nc.vector.tensor_copy if (c, m) in VECTOR_BANKS else nc.scalar.copy
-                    copy(out=result[:, i, :], in_=acc)
-                nc.sync.dma_start(out=out_tiles[:, m0 : m0 + per_store, c0 : c0 + CHUNK], in_=result[:])
+        def skip_product(c0, cols, b, opens):
+            side_by_side(c0, cols, b, w3_codes, w3_scales, skip_words[c0], skip_scales[c0], opens)
+
+        def z_product(c0, cols, b, opens):
+            side_by_side(c0, cols, b, w2_codes, w2_scales, z_codes[c0][:], z_scales[c0][:], opens)
+
+        def low_pair(copy, c0, cols):
+            interleave(copy, grouped[c0][:, :, 0:2], pair_rows(0)[:, :, c0 : c0 + cols])
+
+        z_codes, z_scales = {}, {}
+
+        def quantize_z(c0, cols):
+            z_codes[c0] = sbuf([P, cols], U32, "z_codes%d" % c0)
+            z_scales[c0] = sbuf([P, cols], U8, "z_scales%d" % c0)
+            quantize(z_codes[c0][:], z_scales[c0][:], grouped[c0])
+
+        def store(c0, cols, b):
+            per_bank = M_TILES // len(CHUNK_BANKS[c0])
+            m0 = CHUNK_BANKS[c0].index(b) * per_bank
+            result = sbuf([P, per_bank, cols], F32, "result%d_%d" % (c0, b))
+            copy = nc.vector.tensor_copy if (c0, b) in VECTOR_BANKS else nc.scalar.copy
+            copy(out=result[:].rearrange("p m w -> p (m w)"), in_=banks[c0, b][:, 0 : per_bank * cols])
+            nc.sync.dma_start(out=out_tiles[:, m0 : m0 + per_bank, c0 : c0 + cols], in_=result[:])
+
+        def finish(c0, cols):
+            for b in CHUNK_BANKS[c0]:
+                z_product(c0, cols, b, False)
+                store(c0, cols, b)
+
+        for c0, cols in CHUNKS[:-1]:
+            for b in CHUNK_BANKS[c0]:
+                skip_product(c0, cols, b, True)
+        low_pair(nc.vector.tensor_copy, *CHUNKS[0])
+        low_pair(nc.vector.tensor_copy, *CHUNKS[3])
+        low_pair(nc.scalar.copy, *CHUNKS[1])
+        low_pair(nc.scalar.copy, *CHUNKS[2])
+        for chunk in CHUNKS:
+            quantize_z(*chunk)
+        for chunk in CHUNKS[:-1]:
+            finish(*chunk)
+        gather_skip(skip_scales, scale_table, U8, LATE, CHUNK, after="z_codes256")
+        gather_skip(skip_words, word_table, U32, LATE, CHUNK, after="z_codes512")
+        for b in CHUNK_BANKS[LATE]:
+            z_product(*CHUNKS[3], b, True)
+        for b in CHUNK_BANKS[LATE]:
+            skip_product(*CHUNKS[3], b, False)
+            store(*CHUNKS[3], b)

@@ -74,7 +74,7 @@ def tile_picked_segunpool_none_p_kernel(
         nc.vector.memset(scale_table[:].bitcast(I32), 0)
         w1_raw = sbuf([P, PACK, H], F32, "w1_raw")
         w1_rows = w1.rearrange("(p j) c -> p j c", j=PACK)
-        nc.scalar.dma_start(out=w1_raw[:, 0:2, :], in_=w1_rows[:, 0:2, :])
+        nc.scalar.dma_start(out=w1_raw[:, 0:1, :], in_=w1_rows[:, 0:1, :])
         offs_t = lists.tile([P, S // LIST_ROWS], U16, name="offs_t")
         nc.sync.dma_start(offs_t[:], offs)
         for q in range(QUADRANTS):
@@ -88,7 +88,7 @@ def tile_picked_segunpool_none_p_kernel(
         nc.sync.dma_start(
             out=word_table[:].bitcast(I32), in_=x_words[0].rearrange("p c r -> p (c r)").bitcast(I32)
         )
-        nc.sync.dma_start(out=w1_raw[:, 2:4, :], in_=w1_rows[:, 2:4, :])
+        nc.sync.dma_start(out=w1_raw[:, 1:4, :], in_=w1_rows[:, 1:4, :])
         where_t = lists.tile([P, S // LIST_ROWS], U16, name="where_t")
         nc.sync.dma_start(where_t[:], where)
         w3_raw = sbuf([P, PACK, N], F32, "w3_raw")

@@ -24,6 +24,7 @@ HALF = S // 2
 M_TILES = N // P
 CHUNK = 256
 CHUNKS = tuple((c0, CHUNK) for c0 in range(0, U, CHUNK))
+SPLIT = 320
 LATE = U - CHUNK
 CHUNK_BANKS = {0: (0, 1, 2, 3), 256: (4, 5), 512: (6, 7), 768: (0, 1, 2, 3)}
 VECTOR_BANKS = ((256, 4), (768, 0), (768, 2))
@@ -47,6 +48,7 @@ def tile_picked_segunpool_none_p_kernel(
     with ExitStack() as ctx:
         lists = ctx.enter_context(tc.tile_pool(name="lists", bufs=1))
         keep = ctx.enter_context(tc.tile_pool(name="keep", bufs=1))
+        shared = ctx.enter_context(tc.tile_pool(name="shared", bufs=1))
         psum = ctx.enter_context(tc.psum_pool(name="psum", bufs=1))
 
         def sbuf(shape, dtype, name, after=None):
@@ -99,7 +101,9 @@ def tile_picked_segunpool_none_p_kernel(
             nc.sync.dma_start(out=w2_raw[:, t, :], in_=w2_rows[t])
 
         pairs = {t: sbuf([P, 2 * U], F32, "pair%d" % t) for t in (0, 2)}
-        windows = {t: pairs[t] if t in pairs else sbuf([P, U], F32, "window%d" % t) for t in range(PACK)}
+        windows = dict(pairs)
+        windows[3] = sbuf([P, U], F32, "window3")
+        windows[1] = shared.tile([P, U], F32, name="window1", offset=0, align_bytes=ALIGN)
         zero = sbuf([P, 1], F32, "zero")
         nc.vector.memset(zero[:], 0.0)
         for t in (3, 1):
@@ -162,7 +166,10 @@ def tile_picked_segunpool_none_p_kernel(
         scatter(1, y1, 0, S)
         nc.sync.dma_start(out=pairs[0][:, U : 2 * U], in_=windows[1][:])
         y2 = project(2, 0, S, 4)
-        y0 = project(0, 0, S, 3)
+        y0_bank = bank_tile(3, "y_bank0")
+        product(y0_bank[:], w1_codes[0], w1_scales[0], 0, picked_words[:], picked_scales[:], True, True)
+        y0_low = sbuf([P, SPLIT], F32, "y0_low")
+        nc.scalar.copy(out=y0_low[:], in_=y0_bank[:, 0:SPLIT])
 
         w3_grouped = sbuf([P, N, PACK], BF16, "w3_grouped", after="w1_codes1")
         interleave(nc.scalar.copy, w3_grouped[:], w3_raw[:])
@@ -170,17 +177,20 @@ def tile_picked_segunpool_none_p_kernel(
         interleave(nc.scalar.copy, w2_grouped[:], w2_raw[:])
 
         scatter(2, y2, 0, S)
+        y0_high = shared.tile([P, S - SPLIT], F32, name="y0_high", offset=N, align_bytes=ALIGN)
+        nc.scalar.copy(out=y0_high[:], in_=y0_bank[:, SPLIT:S])
         grouped = {}
         for c0, cols in CHUNKS:
             grouped[c0] = sbuf([P, cols, PACK], BF16, "z_grouped%d" % c0)[:]
             interleave(nc.scalar.copy, grouped[c0][:, :, 2:4], pair_rows(2)[:, :, c0 : c0 + cols])
-        w2_codes = sbuf([P, N], U32, "w2_codes")
-        w2_scales = sbuf([P, N], U8, "w2_scales", after="y1_0")
-        quantize(w2_codes[:], w2_scales[:], w2_grouped[:])
+        scatter(0, y0_low[:], 0, SPLIT)
         w3_codes = sbuf([P, N], U32, "w3_codes")
-        w3_scales = sbuf([P, N], U8, "w3_scales", after="y2_0")
+        w3_scales = shared.tile([P, N], U8, name="w3_scales", offset=0, align_bytes=ALIGN)
         quantize(w3_codes[:], w3_scales[:], w3_grouped[:])
-        scatter(0, y0, 0, S)
+        scatter(0, y0_high[:], SPLIT, S - SPLIT)
+        w2_codes = sbuf([P, N], U32, "w2_codes")
+        w2_scales = sbuf([P, N], U8, "w2_scales", after="y0_low")
+        quantize(w2_codes[:], w2_scales[:], w2_grouped[:])
 
         out_tiles = out.rearrange("(m p) w -> p m w", p=P)
         banks = {}

@@ -49,6 +49,7 @@ def tile_picked_segunpool_none_p_kernel(
         lists = ctx.enter_context(tc.tile_pool(name="lists", bufs=1))
         keep = ctx.enter_context(tc.tile_pool(name="keep", bufs=1))
         shared = ctx.enter_context(tc.tile_pool(name="shared", bufs=1))
+        second = ctx.enter_context(tc.tile_pool(name="second", bufs=1))
         psum = ctx.enter_context(tc.psum_pool(name="psum", bufs=1))
 
         def sbuf(shape, dtype, name, after=None):
@@ -74,15 +75,16 @@ def tile_picked_segunpool_none_p_kernel(
 
         scale_table = sbuf([P, T], U8, "scale_table")
         nc.vector.memset(scale_table[:].bitcast(I32), 0)
-        w1_raw = sbuf([P, PACK, H], F32, "w1_raw")
         w1_rows = w1.rearrange("(p j) c -> p j c", j=PACK)
-        nc.scalar.dma_start(out=w1_raw[:, 0:1, :], in_=w1_rows[:, 0:1, :])
+        w1_left = sbuf([P, PACK, H // 2], F32, "w1_left")
+        w1_right = second.tile([P, PACK, H // 2], F32, name="w1_right", offset=0, align_bytes=ALIGN)
+        nc.scalar.dma_start(out=w1_left[:, 0:2, :], in_=w1_rows[:, 0:2, 0 : H // 2])
         offs_t = lists.tile([P, S // LIST_ROWS], U16, name="offs_t")
         nc.sync.dma_start(offs_t[:], offs)
-        for q in range(QUADRANTS):
+        for r in range(4):
             nc.sync.dma_start(
-                out=scale_table[32 * q : 32 * q + 4, :].bitcast(I32),
-                in_=x_scales[0, 4 * q : 4 * q + 4, :].bitcast(I32),
+                out=scale_table[r:P:32, :].bitcast(I32),
+                in_=x_scales[0, r:16:4, :].bitcast(I32),
             )
         skip_t = lists.tile([P, U // LIST_ROWS], U16, name="skip_t")
         nc.sync.dma_start(skip_t[:], skip)
@@ -90,7 +92,8 @@ def tile_picked_segunpool_none_p_kernel(
         nc.sync.dma_start(
             out=word_table[:].bitcast(I32), in_=x_words[0].rearrange("p c r -> p (c r)").bitcast(I32)
         )
-        nc.sync.dma_start(out=w1_raw[:, 1:4, :], in_=w1_rows[:, 1:4, :])
+        nc.sync.dma_start(out=w1_left[:, 2:4, :], in_=w1_rows[:, 2:4, 0 : H // 2])
+        nc.sync.dma_start(out=w1_right[:], in_=w1_rows[:, :, H // 2 : H])
         where_t = lists.tile([P, S // LIST_ROWS], U16, name="where_t")
         nc.sync.dma_start(where_t[:], where)
         w3_raw = sbuf([P, PACK, N], F32, "w3_raw")
@@ -127,25 +130,31 @@ def tile_picked_segunpool_none_p_kernel(
         picked_words = sbuf([P, S], U32, "picked_words")
         nc.vector.tensor_copy(picked_words[:], word_table[:].indirect(offs_t[:]))
 
-        w1_planes = w1_raw[:].rearrange("p j (b t h i) -> p t b h j i", t=PACK, h=2, i=4)
+        w1_planes = [half[:].rearrange("p j (b t h i) -> p t b h j i", t=PACK, h=2, i=4) for half in (w1_left, w1_right)]
         w1_codes, w1_scales = {}, {}
 
-        def quantize_w1(ts):
+        def quantize_w1(ts, after=None):
             name = "%d" % ts[0]
-            grouped = sbuf([P, len(ts) * P, PACK], BF16, "w1_grouped" + name)
+            grouped = sbuf([P, len(ts) * P, PACK], BF16, "w1_grouped" + name, after=after)
             codes = sbuf([P, len(ts) * P], U32, "w1_codes" + name)
             scales = sbuf([P, len(ts) * P], U8, "w1_scales" + name)
             for n, t in enumerate(ts):
                 cols = slice(n * P, (n + 1) * P)
-                nc.scalar.copy(out=grouped[:, cols, :].rearrange("p (b h i) j -> p b h j i", h=2, i=4), in_=w1_planes[:, t])
+                for side in range(2):
+                    at = n * P + side * P // 2
+                    nc.scalar.copy(
+                        out=grouped[:, at : at + P // 2, :].rearrange("p (b h i) j -> p b h j i", h=2, i=4),
+                        in_=w1_planes[side][:, t],
+                    )
                 w1_codes[t], w1_scales[t] = codes[:, cols], scales[:, cols]
             quantize(codes[:], scales[:], grouped[:])
 
-        def project(t, first, count, b, after=None):
+        def project(t, first, count, b, y=None):
             picked = slice(first, first + count)
             bank = bank_tile(b, "y_bank%d_%d" % (t, first))
             product(bank[:, 0:count], w1_codes[t], w1_scales[t], 0, picked_words[:, picked], picked_scales[:, picked], True, True)
-            y = sbuf([P, count], F32, "y%d_%d" % (t, first), after=after)
+            if y is None:
+                y = sbuf([P, count], F32, "y%d_%d" % (t, first))
             nc.scalar.copy(out=y[:], in_=bank[:, 0:count])
             return y[:]
 
@@ -155,14 +164,17 @@ def tile_picked_segunpool_none_p_kernel(
         def pair_rows(t):
             return pairs[t][:].rearrange("p (t w) -> p t w", t=2)
 
+        gather_skip(skip_words, word_table, U32, 0, CHUNK)
         quantize_w1((3,))
-        y3 = project(3, 0, S, 7)
-        gather_skip(skip_words, word_table, U32, 0, LATE, after="w1_grouped3")
+        y3_low = project(3, 0, HALF, 7)
+        y3_high = project(3, HALF, HALF, 5)
+        gather_skip(skip_words, word_table, U32, CHUNK, LATE - CHUNK, after="w1_grouped3")
         quantize_w1((1,))
-        scatter(3, y3, 0, S)
+        scatter(3, y3_low, 0, HALF)
+        scatter(3, y3_high, HALF, HALF)
         nc.sync.dma_start(out=pairs[2][:, U : 2 * U], in_=windows[3][:])
-        quantize_w1((2, 0))
-        y1 = project(1, 0, S, 6, after="w1_raw")
+        quantize_w1((2, 0), after="w1_codes3")
+        y1 = project(1, 0, S, 6, y=second.tile([P, S], F32, name="y1", offset=0, align_bytes=ALIGN))
         scatter(1, y1, 0, S)
         nc.sync.dma_start(out=pairs[0][:, U : 2 * U], in_=windows[1][:])
         y2 = project(2, 0, S, 4)
@@ -171,7 +183,7 @@ def tile_picked_segunpool_none_p_kernel(
         y0_low = sbuf([P, SPLIT], F32, "y0_low")
         nc.scalar.copy(out=y0_low[:], in_=y0_bank[:, 0:SPLIT])
 
-        w3_grouped = sbuf([P, N, PACK], BF16, "w3_grouped", after="w1_codes1")
+        w3_grouped = second.tile([P, N, PACK], BF16, name="w3_grouped", offset=4 * S, align_bytes=ALIGN)
         interleave(nc.scalar.copy, w3_grouped[:], w3_raw[:])
         w2_grouped = sbuf([P, N, PACK], BF16, "w2_grouped", after="w1_codes2")
         interleave(nc.scalar.copy, w2_grouped[:], w2_raw[:])

@@ -23,11 +23,17 @@ BANK_COLS = 512
 HALF = S // 2
 M_TILES = N // P
 CHUNK = 256
+WIDE = 2 * CHUNK
 CHUNKS = tuple((c0, CHUNK) for c0 in range(0, U, CHUNK))
 SPLIT = 320
 LATE = U - CHUNK
-CHUNK_BANKS = {0: (0, 1, 2, 3), 256: (4, 5), 512: (6, 7), 768: (0, 1, 2, 3)}
-VECTOR_BANKS = ((256, 4), (768, 0), (768, 2))
+CHUNK_BANKS = {
+    0: {0: (0,), 1: (1,), 2: (2, 3)},
+    CHUNK: {3: (0, 1), 4: (2, 3)},
+    WIDE: {5: (0, 1), 6: (2, 3)},
+    LATE: {7: (0, 1), 0: (2,), 1: (3,)},
+}
+VECTOR_BANKS = {(LATE, 7): "result0_0", (LATE, 0): "result0_2"}
 
 
 def entries(list_tile, first, count):
@@ -121,9 +127,8 @@ def tile_picked_segunpool_none_p_kernel(
         def gather_skip(store, table, dtype, first, count, after=None):
             tile = sbuf([P, count], dtype, "skip%d_%d" % (store is skip_words, first), after=after)
             nc.vector.tensor_copy(tile[:], table[:].indirect(entries(skip_t, first, count)))
-            for c0, cols in CHUNKS:
-                if first <= c0 < first + count:
-                    store[c0] = tile[:, c0 - first : c0 - first + cols]
+            for c0 in range(first, first + count, CHUNK):
+                store[c0] = tile[:, c0 - first : c0 - first + CHUNK]
 
         gather_skip(skip_scales, scale_table, U8, 0, LATE)
 
@@ -164,11 +169,10 @@ def tile_picked_segunpool_none_p_kernel(
         def pair_rows(t):
             return pairs[t][:].rearrange("p (t w) -> p t w", t=2)
 
-        gather_skip(skip_words, word_table, U32, 0, CHUNK)
         quantize_w1((3,))
         y3_low = project(3, 0, HALF, 7)
         y3_high = project(3, HALF, HALF, 5)
-        gather_skip(skip_words, word_table, U32, CHUNK, LATE - CHUNK, after="w1_grouped3")
+        gather_skip(skip_words, word_table, U32, 0, WIDE, after="w1_grouped3")
         quantize_w1((1,))
         scatter(3, y3_low, 0, HALF)
         scatter(3, y3_high, HALF, HALF)
@@ -207,21 +211,22 @@ def tile_picked_segunpool_none_p_kernel(
         out_tiles = out.rearrange("(m p) w -> p m w", p=P)
         banks = {}
 
-        def side_by_side(c0, cols, b, w_codes, w_scales, codes, scales, opens):
-            per_bank = M_TILES // len(CHUNK_BANKS[c0])
+        def side_by_side(c0, cols, b, w_codes, w_scales, pieces, opens, closes):
             if opens:
                 banks[c0, b] = bank_tile(b, "out_bank%d_%d" % (c0, b))
-            for i in range(per_bank):
+            passes = [(i, m, piece) for i, m in enumerate(CHUNK_BANKS[c0][b]) for piece in pieces]
+            for n, (i, m, (at, width, codes, scales)) in enumerate(passes):
                 product(
-                    banks[c0, b][:, i * cols : (i + 1) * cols], w_codes, w_scales, CHUNK_BANKS[c0].index(b) * per_bank + i,
-                    codes, scales, opens and i == 0, not opens and i == per_bank - 1,
+                    banks[c0, b][:, i * cols + at : i * cols + at + width], w_codes, w_scales, m,
+                    codes, scales, opens and n == 0, closes and n == len(passes) - 1,
                 )
 
-        def skip_product(c0, cols, b, opens):
-            side_by_side(c0, cols, b, w3_codes, w3_scales, skip_words[c0], skip_scales[c0], opens)
+        def skip_product(c0, cols, b, starts, opens, closes):
+            pieces = [(at, CHUNK, skip_words[c0 + at], skip_scales[c0 + at]) for at in starts]
+            side_by_side(c0, cols, b, w3_codes, w3_scales, pieces, opens, closes)
 
-        def z_product(c0, cols, b, opens):
-            side_by_side(c0, cols, b, w2_codes, w2_scales, z_codes[c0][:], z_scales[c0][:], opens)
+        def z_product(c0, cols, b, opens, closes):
+            side_by_side(c0, cols, b, w2_codes, w2_scales, [(0, cols, z_codes[c0][:], z_scales[c0][:])], opens, closes)
 
         def low_pair(copy, c0, cols):
             interleave(copy, grouped[c0][:, :, 0:2], pair_rows(0)[:, :, c0 : c0 + cols])
@@ -234,33 +239,38 @@ def tile_picked_segunpool_none_p_kernel(
             quantize(z_codes[c0][:], z_scales[c0][:], grouped[c0])
 
         def store(c0, cols, b):
-            per_bank = M_TILES // len(CHUNK_BANKS[c0])
-            m0 = CHUNK_BANKS[c0].index(b) * per_bank
-            result = sbuf([P, per_bank, cols], F32, "result%d_%d" % (c0, b))
+            per_bank = len(CHUNK_BANKS[c0][b])
+            m0 = CHUNK_BANKS[c0][b][0]
+            result = sbuf([P, per_bank, cols], F32, "result%d_%d" % (c0, b), after=VECTOR_BANKS.get((c0, b)))
             copy = nc.vector.tensor_copy if (c0, b) in VECTOR_BANKS else nc.scalar.copy
             copy(out=result[:].rearrange("p m w -> p (m w)"), in_=banks[c0, b][:, 0 : per_bank * cols])
             nc.sync.dma_start(out=out_tiles[:, m0 : m0 + per_bank, c0 : c0 + cols], in_=result[:])
 
         def finish(c0, cols):
             for b in CHUNK_BANKS[c0]:
-                z_product(c0, cols, b, False)
+                z_product(c0, cols, b, False, True)
                 store(c0, cols, b)
 
-        for c0, cols in CHUNKS[:-1]:
+        for c0, cols in CHUNKS[:2]:
             for b in CHUNK_BANKS[c0]:
-                skip_product(c0, cols, b, True)
+                skip_product(c0, cols, b, (0,), True, False)
         low_pair(nc.vector.tensor_copy, *CHUNKS[0])
         low_pair(nc.vector.tensor_copy, *CHUNKS[3])
         low_pair(nc.scalar.copy, *CHUNKS[1])
         low_pair(nc.scalar.copy, *CHUNKS[2])
-        for chunk in CHUNKS:
+        for chunk in CHUNKS[:2]:
             quantize_z(*chunk)
-        for chunk in CHUNKS[:-1]:
             finish(*chunk)
-        gather_skip(skip_scales, scale_table, U8, LATE, CHUNK, after="z_codes256")
-        gather_skip(skip_words, word_table, U32, LATE, CHUNK, after="z_codes512")
+        gather_skip(skip_words, word_table, U32, WIDE, CHUNK, after="z_grouped%d" % CHUNK)
+        for b in CHUNK_BANKS[WIDE]:
+            skip_product(*CHUNKS[2], b, (0,), True, False)
+        quantize_z(*CHUNKS[2])
+        finish(*CHUNKS[2])
+        quantize_z(*CHUNKS[3])
+        gather_skip(skip_scales, scale_table, U8, LATE, CHUNK, after="pair0")
+        gather_skip(skip_words, word_table, U32, LATE, CHUNK, after="z_grouped%d" % WIDE)
         for b in CHUNK_BANKS[LATE]:
-            z_product(*CHUNKS[3], b, True)
+            z_product(*CHUNKS[3], b, True, False)
         for b in CHUNK_BANKS[LATE]:
-            skip_product(*CHUNKS[3], b, False)
+            skip_product(*CHUNKS[3], b, (0,), False, True)
             store(*CHUNKS[3], b)

@@ -25,15 +25,16 @@ M_TILES = N // P
 CHUNK = 256
 WIDE = 2 * CHUNK
 CHUNKS = tuple((c0, CHUNK) for c0 in range(0, U, CHUNK))
+SHARE = 176
 SPLIT = 320
 LATE = U - CHUNK
 CHUNK_BANKS = {
-    0: {0: (0,), 1: (1,), 2: (2, 3)},
-    CHUNK: {3: (0, 1), 4: (2, 3)},
-    WIDE: {5: (0, 1), 6: (2, 3)},
-    LATE: {7: (0, 1), 0: (2,), 1: (3,)},
+    0: {0: (0,), 1: (1,), 2: (2,), 3: (3,)},
+    CHUNK: {4: (0, 1), 5: (2, 3)},
+    WIDE: {6: (0, 1), 7: (2,), 0: (3,)},
+    LATE: {1: (0,), 2: (1,), 3: (2,), 4: (3,)},
 }
-VECTOR_BANKS = {(LATE, 7): "result0_0", (LATE, 0): "result0_2"}
+VECTOR_BANKS = {(0, 2): 0, (WIDE, 0): "result0_0", (LATE, 2): "result0_1", (LATE, 4): "result0_3"}
 
 
 def entries(list_tile, first, count):
@@ -56,9 +57,12 @@ def tile_picked_segunpool_none_p_kernel(
         keep = ctx.enter_context(tc.tile_pool(name="keep", bufs=1))
         shared = ctx.enter_context(tc.tile_pool(name="shared", bufs=1))
         second = ctx.enter_context(tc.tile_pool(name="second", bufs=1))
+        third = ctx.enter_context(tc.tile_pool(name="third", bufs=1))
         psum = ctx.enter_context(tc.psum_pool(name="psum", bufs=1))
 
         def sbuf(shape, dtype, name, after=None):
+            if isinstance(after, int):
+                return third.tile(shape, dtype, name=name, offset=after * 4 * CHUNK, align_bytes=ALIGN)
             return keep.tile(shape, dtype, name=name, tag=after or name, align_bytes=ALIGN)
 
         def bank_tile(b, name):
@@ -88,7 +92,7 @@ def tile_picked_segunpool_none_p_kernel(
         offs_t = lists.tile([P, S // LIST_ROWS], U16, name="offs_t")
         nc.sync.dma_start(offs_t[:], offs)
         for r in range(4):
-            nc.sync.dma_start(
+            (nc.sync if r % 2 == 0 else nc.scalar).dma_start(
                 out=scale_table[r:P:32, :].bitcast(I32),
                 in_=x_scales[0, r:16:4, :].bitcast(I32),
             )
@@ -109,7 +113,10 @@ def tile_picked_segunpool_none_p_kernel(
         for t in range(PACK):
             nc.sync.dma_start(out=w2_raw[:, t, :], in_=w2_rows[t])
 
-        pairs = {t: sbuf([P, 2 * U], F32, "pair%d" % t) for t in (0, 2)}
+        pairs = {
+            0: third.tile([P, 2 * U], F32, name="pair0", offset=0, align_bytes=ALIGN),
+            2: sbuf([P, 2 * U], F32, "pair2"),
+        }
         windows = dict(pairs)
         windows[3] = sbuf([P, U], F32, "window3")
         windows[1] = shared.tile([P, U], F32, name="window1", offset=0, align_bytes=ALIGN)
@@ -159,9 +166,9 @@ def tile_picked_segunpool_none_p_kernel(
             bank = bank_tile(b, "y_bank%d_%d" % (t, first))
             product(bank[:, 0:count], w1_codes[t], w1_scales[t], 0, picked_words[:, picked], picked_scales[:, picked], True, True)
             if y is None:
-                y = sbuf([P, count], F32, "y%d_%d" % (t, first))
-            nc.scalar.copy(out=y[:], in_=bank[:, 0:count])
-            return y[:]
+                y = sbuf([P, count], F32, "y%d_%d" % (t, first))[:]
+            nc.scalar.copy(out=y, in_=bank[:, 0:count])
+            return y
 
         def scatter(t, y, first, count):
             nc.vector.tensor_copy(windows[t][:].indirect(entries(where_t, first, count)), y)
@@ -170,15 +177,15 @@ def tile_picked_segunpool_none_p_kernel(
             return pairs[t][:].rearrange("p (t w) -> p t w", t=2)
 
         quantize_w1((3,))
-        y3_low = project(3, 0, HALF, 7)
-        y3_high = project(3, HALF, HALF, 5)
-        gather_skip(skip_words, word_table, U32, 0, WIDE, after="w1_grouped3")
+        y3 = sbuf([P, S], F32, "y3")
+        project(3, 0, HALF, 7, y=y3[:, 0:HALF])
+        project(3, HALF, HALF, 5, y=y3[:, HALF:S])
         quantize_w1((1,))
-        scatter(3, y3_low, 0, HALF)
-        scatter(3, y3_high, HALF, HALF)
+        gather_skip(skip_words, word_table, U32, 0, WIDE, after="w1_grouped3")
+        scatter(3, y3[:], 0, S)
         nc.sync.dma_start(out=pairs[2][:, U : 2 * U], in_=windows[3][:])
         quantize_w1((2, 0), after="w1_codes3")
-        y1 = project(1, 0, S, 6, y=second.tile([P, S], F32, name="y1", offset=0, align_bytes=ALIGN))
+        y1 = project(1, 0, S, 6, y=second.tile([P, S], F32, name="y1", offset=0, align_bytes=ALIGN)[:])
         scatter(1, y1, 0, S)
         nc.sync.dma_start(out=pairs[0][:, U : 2 * U], in_=windows[1][:])
         y2 = project(2, 0, S, 4)
@@ -228,8 +235,8 @@ def tile_picked_segunpool_none_p_kernel(
         def z_product(c0, cols, b, opens, closes):
             side_by_side(c0, cols, b, w2_codes, w2_scales, [(0, cols, z_codes[c0][:], z_scales[c0][:])], opens, closes)
 
-        def low_pair(copy, c0, cols):
-            interleave(copy, grouped[c0][:, :, 0:2], pair_rows(0)[:, :, c0 : c0 + cols])
+        def low_pair(copy, c0, first, stop):
+            interleave(copy, grouped[c0][:, first:stop, 0:2], pair_rows(0)[:, :, c0 + first : c0 + stop])
 
         z_codes, z_scales = {}, {}
 
@@ -254,23 +261,21 @@ def tile_picked_segunpool_none_p_kernel(
         for c0, cols in CHUNKS[:2]:
             for b in CHUNK_BANKS[c0]:
                 skip_product(c0, cols, b, (0,), True, False)
-        low_pair(nc.vector.tensor_copy, *CHUNKS[0])
-        low_pair(nc.vector.tensor_copy, *CHUNKS[3])
-        low_pair(nc.scalar.copy, *CHUNKS[1])
-        low_pair(nc.scalar.copy, *CHUNKS[2])
+        low_pair(nc.vector.tensor_copy, 0, 0, CHUNK)
+        low_pair(nc.vector.tensor_copy, LATE, 0, SHARE)
+        low_pair(nc.scalar.copy, CHUNK, 0, CHUNK)
+        low_pair(nc.scalar.copy, LATE, SHARE, CHUNK)
+        low_pair(nc.scalar.copy, WIDE, 0, CHUNK)
+        for c in (0, 1, 3, 2):
+            quantize_z(*CHUNKS[c])
         for chunk in CHUNKS[:2]:
-            quantize_z(*chunk)
             finish(*chunk)
-        gather_skip(skip_words, word_table, U32, WIDE, CHUNK, after="z_grouped%d" % CHUNK)
-        for b in CHUNK_BANKS[WIDE]:
-            skip_product(*CHUNKS[2], b, (0,), True, False)
-        quantize_z(*CHUNKS[2])
-        finish(*CHUNKS[2])
-        quantize_z(*CHUNKS[3])
-        gather_skip(skip_scales, scale_table, U8, LATE, CHUNK, after="pair0")
-        gather_skip(skip_words, word_table, U32, LATE, CHUNK, after="z_grouped%d" % WIDE)
-        for b in CHUNK_BANKS[LATE]:
-            z_product(*CHUNKS[3], b, True, False)
-        for b in CHUNK_BANKS[LATE]:
-            skip_product(*CHUNKS[3], b, (0,), False, True)
-            store(*CHUNKS[3], b)
+        gather_skip(skip_words, word_table, U32, WIDE, CHUNK, after=1)
+        gather_skip(skip_scales, scale_table, U8, LATE, CHUNK, after=2)
+        gather_skip(skip_words, word_table, U32, LATE, CHUNK, after=3)
+        for c0, cols in CHUNKS[2:]:
+            for b in CHUNK_BANKS[c0]:
+                z_product(c0, cols, b, True, False)
+            for b in CHUNK_BANKS[c0]:
+                skip_product(c0, cols, b, (0,), False, True)
+                store(c0, cols, b)

@@ -92,7 +92,7 @@ def tile_picked_segunpool_none_p_kernel(
         offs_t = lists.tile([P, S // LIST_ROWS], U16, name="offs_t")
         nc.sync.dma_start(offs_t[:], offs)
         for r in range(4):
-            (nc.sync if r % 2 == 0 else nc.scalar).dma_start(
+            nc.sync.dma_start(
                 out=scale_table[r:P:32, :].bitcast(I32),
                 in_=x_scales[0, r:16:4, :].bitcast(I32),
             )

@@ -56,7 +56,6 @@ def tile_picked_segunpool_none_p_kernel(
         lists = ctx.enter_context(tc.tile_pool(name="lists", bufs=1))
         keep = ctx.enter_context(tc.tile_pool(name="keep", bufs=1))
         shared = ctx.enter_context(tc.tile_pool(name="shared", bufs=1))
-        second = ctx.enter_context(tc.tile_pool(name="second", bufs=1))
         third = ctx.enter_context(tc.tile_pool(name="third", bufs=1))
         psum = ctx.enter_context(tc.psum_pool(name="psum", bufs=1))
 
@@ -86,9 +85,8 @@ def tile_picked_segunpool_none_p_kernel(
         scale_table = sbuf([P, T], U8, "scale_table")
         nc.vector.memset(scale_table[:].bitcast(I32), 0)
         w1_rows = w1.rearrange("(p j) c -> p j c", j=PACK)
-        w1_left = sbuf([P, PACK, H // 2], F32, "w1_left")
-        w1_right = second.tile([P, PACK, H // 2], F32, name="w1_right", offset=0, align_bytes=ALIGN)
-        nc.scalar.dma_start(out=w1_left[:, 0:2, :], in_=w1_rows[:, 0:2, 0 : H // 2])
+        w1_raw = sbuf([P, PACK, H], F32, "w1_raw")
+        nc.scalar.dma_start(out=w1_raw[:, 0:1, :], in_=w1_rows[:, 0:1, :])
         offs_t = lists.tile([P, S // LIST_ROWS], U16, name="offs_t")
         nc.sync.dma_start(offs_t[:], offs)
         for r in range(4):
@@ -98,12 +96,11 @@ def tile_picked_segunpool_none_p_kernel(
             )
         skip_t = lists.tile([P, U // LIST_ROWS], U16, name="skip_t")
         nc.sync.dma_start(skip_t[:], skip)
+        nc.sync.dma_start(out=w1_raw[:, 1:PACK, :], in_=w1_rows[:, 1:PACK, :])
         word_table = sbuf([P, T], U32, "word_table")
         nc.sync.dma_start(
             out=word_table[:].bitcast(I32), in_=x_words[0].rearrange("p c r -> p (c r)").bitcast(I32)
         )
-        nc.sync.dma_start(out=w1_left[:, 2:4, :], in_=w1_rows[:, 2:4, 0 : H // 2])
-        nc.sync.dma_start(out=w1_right[:], in_=w1_rows[:, :, H // 2 : H])
         where_t = lists.tile([P, S // LIST_ROWS], U16, name="where_t")
         nc.sync.dma_start(where_t[:], where)
         w3_raw = sbuf([P, PACK, N], F32, "w3_raw")
@@ -139,10 +136,7 @@ def tile_picked_segunpool_none_p_kernel(
 
         gather_skip(skip_scales, scale_table, U8, 0, LATE)
 
-        picked_words = sbuf([P, S], U32, "picked_words")
-        nc.vector.tensor_copy(picked_words[:], word_table[:].indirect(offs_t[:]))
-
-        w1_planes = [half[:].rearrange("p j (b t h i) -> p t b h j i", t=PACK, h=2, i=4) for half in (w1_left, w1_right)]
+        w1_planes = w1_raw[:].rearrange("p j (b t h i) -> p t b h j i", t=PACK, h=2, i=4)
         w1_codes, w1_scales = {}, {}
 
         def quantize_w1(ts, after=None):
@@ -152,12 +146,9 @@ def tile_picked_segunpool_none_p_kernel(
             scales = sbuf([P, len(ts) * P], U8, "w1_scales" + name)
             for n, t in enumerate(ts):
                 cols = slice(n * P, (n + 1) * P)
-                for side in range(2):
-                    at = n * P + side * P // 2
-                    nc.scalar.copy(
-                        out=grouped[:, at : at + P // 2, :].rearrange("p (b h i) j -> p b h j i", h=2, i=4),
-                        in_=w1_planes[side][:, t],
-                    )
+                nc.scalar.copy(
+                    out=grouped[:, cols, :].rearrange("p (b h i) j -> p b h j i", h=2, i=4), in_=w1_planes[:, t]
+                )
                 w1_codes[t], w1_scales[t] = codes[:, cols], scales[:, cols]
             quantize(codes[:], scales[:], grouped[:])
 
@@ -176,16 +167,18 @@ def tile_picked_segunpool_none_p_kernel(
         def pair_rows(t):
             return pairs[t][:].rearrange("p (t w) -> p t w", t=2)
 
-        quantize_w1((3,))
+        quantize_w1((3, 1))
+        picked_words = sbuf([P, S], U32, "picked_words")
+        for first in (0, HALF):
+            nc.vector.tensor_copy(picked_words[:, first : first + HALF], word_table[:].indirect(entries(offs_t, first, HALF)))
+        quantize_w1((2, 0), after="w1_grouped3")
         y3 = sbuf([P, S], F32, "y3")
         project(3, 0, HALF, 7, y=y3[:, 0:HALF])
         project(3, HALF, HALF, 5, y=y3[:, HALF:S])
-        quantize_w1((1,))
-        gather_skip(skip_words, word_table, U32, 0, WIDE, after="w1_grouped3")
+        gather_skip(skip_words, word_table, U32, 0, WIDE)
         scatter(3, y3[:], 0, S)
         nc.sync.dma_start(out=pairs[2][:, U : 2 * U], in_=windows[3][:])
-        quantize_w1((2, 0), after="w1_codes3")
-        y1 = project(1, 0, S, 6, y=second.tile([P, S], F32, name="y1", offset=0, align_bytes=ALIGN)[:])
+        y1 = project(1, 0, S, 6)
         scatter(1, y1, 0, S)
         nc.sync.dma_start(out=pairs[0][:, U : 2 * U], in_=windows[1][:])
         y2 = project(2, 0, S, 4)
@@ -194,9 +187,9 @@ def tile_picked_segunpool_none_p_kernel(
         y0_low = sbuf([P, SPLIT], F32, "y0_low")
         nc.scalar.copy(out=y0_low[:], in_=y0_bank[:, 0:SPLIT])
 
-        w3_grouped = second.tile([P, N, PACK], BF16, name="w3_grouped", offset=4 * S, align_bytes=ALIGN)
+        w3_grouped = sbuf([P, N, PACK], BF16, "w3_grouped", after="w1_codes2")
         interleave(nc.scalar.copy, w3_grouped[:], w3_raw[:])
-        w2_grouped = sbuf([P, N, PACK], BF16, "w2_grouped", after="w1_codes2")
+        w2_grouped = sbuf([P, N, PACK], BF16, "w2_grouped", after="y3")
         interleave(nc.scalar.copy, w2_grouped[:], w2_raw[:])
 
         scatter(2, y2, 0, S)

@@ -28,13 +28,10 @@ CHUNKS = tuple((c0, CHUNK) for c0 in range(0, U, CHUNK))
 SHARE = 176
 SPLIT = 320
 LATE = U - CHUNK
-CHUNK_BANKS = {
-    0: {0: (0,), 1: (1,), 2: (2,), 3: (3,)},
-    CHUNK: {4: (0, 1), 5: (2, 3)},
-    WIDE: {6: (0, 1), 7: (2,), 0: (3,)},
-    LATE: {1: (0,), 2: (1,), 3: (2,), 4: (3,)},
-}
-VECTOR_BANKS = {(0, 2): 0, (WIDE, 0): "result0_0", (LATE, 2): "result0_1", (LATE, 4): "result0_3"}
+STORES = (
+    (0, 0, 1, 0), (1, 0, 1, 1), (2, 0, 2, 2), (3, 0, 2, 3),
+    (0, 1, 2, 4), (1, 1, 2, 5), (0, 3, 1, 0), (1, 3, 1, 1), (2, 2, 2, 6), (3, 2, 2, 7),
+)
 
 
 def entries(list_tile, first, count):
@@ -132,7 +129,7 @@ def tile_picked_segunpool_none_p_kernel(
             tile = sbuf([P, count], dtype, "skip%d_%d" % (store is skip_words, first), after=after)
             nc.vector.tensor_copy(tile[:], table[:].indirect(entries(skip_t, first, count)))
             for c0 in range(first, first + count, CHUNK):
-                store[c0] = tile[:, c0 - first : c0 - first + CHUNK]
+                store[c0] = tile[:, c0 - first : count]
 
         gather_skip(skip_scales, scale_table, U8, 0, LATE)
 
@@ -173,16 +170,16 @@ def tile_picked_segunpool_none_p_kernel(
             nc.vector.tensor_copy(picked_words[:, first : first + HALF], word_table[:].indirect(entries(offs_t, first, HALF)))
         quantize_w1((2, 0), after="w1_grouped3")
         y3 = sbuf([P, S], F32, "y3")
-        project(3, 0, HALF, 7, y=y3[:, 0:HALF])
+        project(3, 0, HALF, 4, y=y3[:, 0:HALF])
         project(3, HALF, HALF, 5, y=y3[:, HALF:S])
         gather_skip(skip_words, word_table, U32, 0, WIDE)
         scatter(3, y3[:], 0, S)
         nc.sync.dma_start(out=pairs[2][:, U : 2 * U], in_=windows[3][:])
-        y1 = project(1, 0, S, 6)
+        y1 = project(1, 0, S, 3)
         scatter(1, y1, 0, S)
         nc.sync.dma_start(out=pairs[0][:, U : 2 * U], in_=windows[1][:])
-        y2 = project(2, 0, S, 4)
-        y0_bank = bank_tile(3, "y_bank0")
+        y2 = project(2, 0, S, 6)
+        y0_bank = bank_tile(7, "y_bank0")
         product(y0_bank[:], w1_codes[0], w1_scales[0], 0, picked_words[:], picked_scales[:], True, True)
         y0_low = sbuf([P, SPLIT], F32, "y0_low")
         nc.scalar.copy(out=y0_low[:], in_=y0_bank[:, 0:SPLIT])
@@ -209,66 +206,75 @@ def tile_picked_segunpool_none_p_kernel(
         quantize(w2_codes[:], w2_scales[:], w2_grouped[:])
 
         out_tiles = out.rearrange("(m p) w -> p m w", p=P)
-        banks = {}
+        banks, passes_left = {}, {}
 
-        def side_by_side(c0, cols, b, w_codes, w_scales, pieces, opens, closes):
+        def add(n, c, chunks, w_codes, w_scales, codes, scales):
+            m, first, count, b = STORES[n]
+            opens = n not in banks
             if opens:
-                banks[c0, b] = bank_tile(b, "out_bank%d_%d" % (c0, b))
-            passes = [(i, m, piece) for i, m in enumerate(CHUNK_BANKS[c0][b]) for piece in pieces]
-            for n, (i, m, (at, width, codes, scales)) in enumerate(passes):
-                product(
-                    banks[c0, b][:, i * cols + at : i * cols + at + width], w_codes, w_scales, m,
-                    codes, scales, opens and n == 0, closes and n == len(passes) - 1,
-                )
+                banks[n] = bank_tile(b, "out_bank%d" % n)
+                passes_left[n] = 2 * count
+            passes_left[n] = passes_left[n] - chunks
+            at, cols = (c - first) * CHUNK, chunks * CHUNK
+            product(
+                banks[n][:, at : at + cols], w_codes, w_scales, m,
+                codes[:, 0:cols], scales[:, 0:cols], opens, passes_left[n] == 0,
+            )
 
-        def skip_product(c0, cols, b, starts, opens, closes):
-            pieces = [(at, CHUNK, skip_words[c0 + at], skip_scales[c0 + at]) for at in starts]
-            side_by_side(c0, cols, b, w3_codes, w3_scales, pieces, opens, closes)
+        def stores_with(c):
+            return [n for n, (m, first, count, b) in enumerate(STORES) if first <= c < first + count]
 
-        def z_product(c0, cols, b, opens, closes):
-            side_by_side(c0, cols, b, w2_codes, w2_scales, [(0, cols, z_codes[c0][:], z_scales[c0][:])], opens, closes)
+        def skip_product(n, c, chunks=1):
+            add(n, c, chunks, w3_codes, w3_scales, skip_words[c * CHUNK], skip_scales[c * CHUNK])
+
+        def z_product(n, c):
+            add(n, c, 1, w2_codes, w2_scales, z_codes[c][:], z_scales[c][:])
 
         def low_pair(copy, c0, first, stop):
             interleave(copy, grouped[c0][:, first:stop, 0:2], pair_rows(0)[:, :, c0 + first : c0 + stop])
 
         z_codes, z_scales = {}, {}
 
-        def quantize_z(c0, cols):
-            z_codes[c0] = sbuf([P, cols], U32, "z_codes%d" % c0)
-            z_scales[c0] = sbuf([P, cols], U8, "z_scales%d" % c0)
-            quantize(z_codes[c0][:], z_scales[c0][:], grouped[c0])
+        def quantize_z(c):
+            z_codes[c] = sbuf([P, CHUNK], U32, "z_codes%d" % c)
+            z_scales[c] = sbuf([P, CHUNK], U8, "z_scales%d" % c)
+            quantize(z_codes[c][:], z_scales[c][:], grouped[c * CHUNK])
 
-        def store(c0, cols, b):
-            per_bank = len(CHUNK_BANKS[c0][b])
-            m0 = CHUNK_BANKS[c0][b][0]
-            result = sbuf([P, per_bank, cols], F32, "result%d_%d" % (c0, b), after=VECTOR_BANKS.get((c0, b)))
-            copy = nc.vector.tensor_copy if (c0, b) in VECTOR_BANKS else nc.scalar.copy
-            copy(out=result[:].rearrange("p m w -> p (m w)"), in_=banks[c0, b][:, 0 : per_bank * cols])
-            nc.sync.dma_start(out=out_tiles[:, m0 : m0 + per_bank, c0 : c0 + cols], in_=result[:])
+        def store(n):
+            m, first, count, b = STORES[n]
+            last = n >= len(STORES) - 2
+            cols = count * CHUNK
+            result = sbuf([P, cols], F32, "result%d" % n, after="result%d" % (n - 7) if last else None)
+            copy = nc.vector.tensor_copy if last else nc.scalar.copy
+            copy(out=result[:], in_=banks[n][:, 0:cols])
+            nc.sync.dma_start(out=out_tiles[:, m, first * CHUNK : first * CHUNK + cols], in_=result[:])
 
-        def finish(c0, cols):
-            for b in CHUNK_BANKS[c0]:
-                z_product(c0, cols, b, False, True)
-                store(c0, cols, b)
-
-        for c0, cols in CHUNKS[:2]:
-            for b in CHUNK_BANKS[c0]:
-                skip_product(c0, cols, b, (0,), True, False)
+        for n, (m, first, count, b) in enumerate(STORES):
+            if first < 2:
+                skip_product(n, first, min(count, 2 - first))
         low_pair(nc.vector.tensor_copy, 0, 0, CHUNK)
         low_pair(nc.vector.tensor_copy, LATE, 0, SHARE)
         low_pair(nc.scalar.copy, CHUNK, 0, CHUNK)
         low_pair(nc.scalar.copy, LATE, SHARE, CHUNK)
         low_pair(nc.scalar.copy, WIDE, 0, CHUNK)
         for c in (0, 1, 3, 2):
-            quantize_z(*CHUNKS[c])
-        for chunk in CHUNKS[:2]:
-            finish(*chunk)
+            quantize_z(c)
+        for c in (0, 1):
+            for n in stores_with(c):
+                z_product(n, c)
+                if passes_left[n] == 0:
+                    store(n)
         gather_skip(skip_words, word_table, U32, WIDE, CHUNK, after=1)
         gather_skip(skip_scales, scale_table, U8, LATE, CHUNK, after=2)
         gather_skip(skip_words, word_table, U32, LATE, CHUNK, after=3)
-        for c0, cols in CHUNKS[2:]:
-            for b in CHUNK_BANKS[c0]:
-                z_product(c0, cols, b, True, False)
-            for b in CHUNK_BANKS[c0]:
-                skip_product(c0, cols, b, (0,), False, True)
-                store(c0, cols, b)
+        for n in (8, 9):
+            z_product(n, 3)
+        for n in stores_with(2):
+            z_product(n, 2)
+        for n in (6, 7):
+            z_product(n, 3)
+        for c in (2, 3):
+            for n in stores_with(c):
+                skip_product(n, c)
+                if passes_left[n] == 0:
+                    store(n)

@@ -32,6 +32,7 @@ STORES = (
     (0, 0, 1, 0), (1, 0, 1, 1), (2, 0, 2, 2), (3, 0, 2, 3),
     (0, 1, 2, 4), (1, 1, 2, 5), (0, 3, 1, 0), (1, 3, 1, 1), (2, 2, 2, 6), (3, 2, 2, 7),
 )
+VECTOR_STORES = {8: "result1", 9: "result2"}
 
 
 def entries(list_tile, first, count):
@@ -227,27 +228,29 @@ def tile_picked_segunpool_none_p_kernel(
         def skip_product(n, c, chunks=1):
             add(n, c, chunks, w3_codes, w3_scales, skip_words[c * CHUNK], skip_scales[c * CHUNK])
 
-        def z_product(n, c):
-            add(n, c, 1, w2_codes, w2_scales, z_codes[c][:], z_scales[c][:])
+        def z_product(n, c, chunks=1):
+            add(n, c, chunks, w2_codes, w2_scales, z_codes[c], z_scales[:, c * CHUNK : U])
 
         def low_pair(copy, c0, first, stop):
             interleave(copy, grouped[c0][:, first:stop, 0:2], pair_rows(0)[:, :, c0 + first : c0 + stop])
 
-        z_codes, z_scales = {}, {}
+        early_codes = sbuf([P, LATE], U32, "early_codes")
+        late_codes = sbuf([P, CHUNK], U32, "late_codes", after=4)
+        z_codes = [early_codes[:, c0:LATE] for c0 in range(0, LATE, CHUNK)] + [late_codes[:]]
+        z_scales = sbuf([P, U], U8, "z_scales")
 
         def quantize_z(c):
-            z_codes[c] = sbuf([P, CHUNK], U32, "z_codes%d" % c)
-            z_scales[c] = sbuf([P, CHUNK], U8, "z_scales%d" % c)
-            quantize(z_codes[c][:], z_scales[c][:], grouped[c * CHUNK])
+            cols = slice(c * CHUNK, (c + 1) * CHUNK)
+            quantize(z_codes[c][:, 0:CHUNK], z_scales[:, cols], grouped[c * CHUNK])
 
         def store(n):
             m, first, count, b = STORES[n]
-            last = n >= len(STORES) - 2
             cols = count * CHUNK
-            result = sbuf([P, cols], F32, "result%d" % n, after="result%d" % (n - 7) if last else None)
-            copy = nc.vector.tensor_copy if last else nc.scalar.copy
+            result = sbuf([P, cols], F32, "result%d" % n, after=VECTOR_STORES.get(n))
+            copy = nc.vector.tensor_copy if n in VECTOR_STORES else nc.scalar.copy
             copy(out=result[:], in_=banks[n][:, 0:cols])
-            nc.sync.dma_start(out=out_tiles[:, m, first * CHUNK : first * CHUNK + cols], in_=result[:])
+            queue = nc.scalar if n in VECTOR_STORES else nc.sync
+            queue.dma_start(out=out_tiles[:, m, first * CHUNK : first * CHUNK + cols], in_=result[:])
 
         for n, (m, first, count, b) in enumerate(STORES):
             if first < 2:
@@ -255,26 +258,32 @@ def tile_picked_segunpool_none_p_kernel(
         low_pair(nc.vector.tensor_copy, 0, 0, CHUNK)
         low_pair(nc.vector.tensor_copy, LATE, 0, SHARE)
         low_pair(nc.scalar.copy, CHUNK, 0, CHUNK)
-        low_pair(nc.scalar.copy, LATE, SHARE, CHUNK)
         low_pair(nc.scalar.copy, WIDE, 0, CHUNK)
-        for c in (0, 1, 3, 2):
+        low_pair(nc.scalar.copy, LATE, SHARE, CHUNK)
+        for c in (0, 1, 2):
             quantize_z(c)
-        for c in (0, 1):
-            for n in stores_with(c):
-                z_product(n, c)
-                if passes_left[n] == 0:
-                    store(n)
+        for n in (0, 1):
+            z_product(n, 0)
+            store(n)
+        z_product(2, 0)
+        z_product(2, 1)
+        store(2)
+        z_product(3, 0, 2)
+        store(3)
+        for n in (4, 5):
+            z_product(n, 1)
         gather_skip(skip_words, word_table, U32, WIDE, CHUNK, after=1)
+        quantize_z(3)
         gather_skip(skip_scales, scale_table, U8, LATE, CHUNK, after=2)
         gather_skip(skip_words, word_table, U32, LATE, CHUNK, after=3)
-        for n in (8, 9):
-            z_product(n, 3)
         for n in stores_with(2):
             z_product(n, 2)
-        for n in (6, 7):
+        for n in stores_with(2):
+            skip_product(n, 2)
+            if passes_left[n] == 0:
+                store(n)
+        for n in stores_with(3):
             z_product(n, 3)
-        for c in (2, 3):
-            for n in stores_with(c):
-                skip_product(n, c)
-                if passes_left[n] == 0:
-                    store(n)
+        for n in stores_with(3):
+            skip_product(n, 3)
+            store(n)

@@ -25,6 +25,7 @@ M_TILES = N // P
 CHUNK = 256
 WIDE = 2 * CHUNK
 CHUNKS = tuple((c0, CHUNK) for c0 in range(0, U, CHUNK))
+EARLY = 704
 SHARE = 176
 SPLIT = 320
 LATE = U - CHUNK
@@ -82,9 +83,9 @@ def tile_picked_segunpool_none_p_kernel(
 
         scale_table = sbuf([P, T], U8, "scale_table")
         nc.vector.memset(scale_table[:].bitcast(I32), 0)
-        w1_rows = w1.rearrange("(p j) c -> p j c", j=PACK)
-        w1_raw = sbuf([P, PACK, H], F32, "w1_raw")
-        nc.scalar.dma_start(out=w1_raw[:, 0:1, :], in_=w1_rows[:, 0:1, :])
+        w1_rows = w1.rearrange("(p j) c -> p (j c)", j=PACK)
+        w1_raw = sbuf([P, PACK * H], F32, "w1_raw")
+        nc.scalar.dma_start(out=w1_raw[:, 0:EARLY], in_=w1_rows[:, 0:EARLY])
         offs_t = lists.tile([P, S // LIST_ROWS], U16, name="offs_t")
         nc.sync.dma_start(offs_t[:], offs)
         for r in range(4):
@@ -94,7 +95,7 @@ def tile_picked_segunpool_none_p_kernel(
             )
         skip_t = lists.tile([P, U // LIST_ROWS], U16, name="skip_t")
         nc.sync.dma_start(skip_t[:], skip)
-        nc.sync.dma_start(out=w1_raw[:, 1:PACK, :], in_=w1_rows[:, 1:PACK, :])
+        nc.sync.dma_start(out=w1_raw[:, EARLY : PACK * H], in_=w1_rows[:, EARLY : PACK * H])
         word_table = sbuf([P, T], U32, "word_table")
         nc.sync.dma_start(
             out=word_table[:].bitcast(I32), in_=x_words[0].rearrange("p c r -> p (c r)").bitcast(I32)
@@ -134,7 +135,7 @@ def tile_picked_segunpool_none_p_kernel(
 
         gather_skip(skip_scales, scale_table, U8, 0, LATE)
 
-        w1_planes = w1_raw[:].rearrange("p j (b t h i) -> p t b h j i", t=PACK, h=2, i=4)
+        w1_planes = w1_raw[:].rearrange("p (j b t h i) -> p t b h j i", j=PACK, t=PACK, h=2, i=4)
         w1_codes, w1_scales = {}, {}
 
         def quantize_w1(ts, after=None):
@@ -243,12 +244,15 @@ def tile_picked_segunpool_none_p_kernel(
             cols = slice(c * CHUNK, (c + 1) * CHUNK)
             quantize(z_codes[c][:, 0:CHUNK], z_scales[:, cols], grouped[c * CHUNK])
 
+        results = {}
+
         def store(n):
             m, first, count, b = STORES[n]
             cols = count * CHUNK
             result = sbuf([P, cols], F32, "result%d" % n, after=VECTOR_STORES.get(n))
             copy = nc.vector.tensor_copy if n in VECTOR_STORES else nc.scalar.copy
             copy(out=result[:], in_=banks[n][:, 0:cols])
+            results[n] = result
             queue = nc.scalar if n in VECTOR_STORES else nc.sync
             queue.dma_start(out=out_tiles[:, m, first * CHUNK : first * CHUNK + cols], in_=result[:])
 

@@ -12,28 +12,25 @@ U32 = mybir.dt.uint32
 U16 = mybir.dt.uint16
 U8 = mybir.dt.uint8
 FP8X4 = mybir.dt.float8_e4m3fn_x4
+COPY = mybir.ActivationFunctionType.Copy
+MULT, ADD = mybir.AluOpType.mult, mybir.AluOpType.add
 
 P = 128
 PACK = 4
-QUADRANTS = 4
 LIST_ROWS = 16
 ALIGN = 64
-BANKS = 8
 BANK_COLS = 512
 HALF = S // 2
-M_TILES = N // P
 CHUNK = 256
-WIDE = 2 * CHUNK
-CHUNKS = tuple((c0, CHUNK) for c0 in range(0, U, CHUNK))
 EARLY = 704
-SHARE = 176
-SPLIT = 320
+SPLIT = 384
 LATE = U - CHUNK
 STORES = (
-    (0, 0, 1, 0), (1, 0, 1, 1), (2, 0, 2, 2), (3, 0, 2, 3),
-    (0, 1, 2, 4), (1, 1, 2, 5), (0, 3, 1, 0), (1, 3, 1, 1), (2, 2, 2, 6), (3, 2, 2, 7),
+    (0, ((0, 0),)), (1, ((1, 0),)), (2, ((2, 0), (3, 0))), (3, ((0, 1), (1, 1))), (4, ((2, 1), (3, 1))),
+    (5, ((0, 2), (1, 2))), (0, ((2, 2), (3, 2))), (6, ((0, 3), (1, 3))), (7, ((2, 3), (3, 3))),
 )
-VECTOR_STORES = {8: "result1", 9: "result2"}
+VECTOR_STORES = (6, 8)
+HELD_STORE = 6
 
 
 def entries(list_tile, first, count):
@@ -54,13 +51,12 @@ def tile_picked_segunpool_none_p_kernel(
     with ExitStack() as ctx:
         lists = ctx.enter_context(tc.tile_pool(name="lists", bufs=1))
         keep = ctx.enter_context(tc.tile_pool(name="keep", bufs=1))
-        shared = ctx.enter_context(tc.tile_pool(name="shared", bufs=1))
-        third = ctx.enter_context(tc.tile_pool(name="third", bufs=1))
+        placed = ctx.enter_context(tc.tile_pool(name="placed", bufs=1))
         psum = ctx.enter_context(tc.psum_pool(name="psum", bufs=1))
 
         def sbuf(shape, dtype, name, after=None):
             if isinstance(after, int):
-                return third.tile(shape, dtype, name=name, offset=after * 4 * CHUNK, align_bytes=ALIGN)
+                return placed.tile(shape, dtype, name=name, offset=after * 4 * CHUNK, align_bytes=ALIGN)
             return keep.tile(shape, dtype, name=name, tag=after or name, align_bytes=ALIGN)
 
         def bank_tile(b, name):
@@ -109,31 +105,31 @@ def tile_picked_segunpool_none_p_kernel(
         for t in range(PACK):
             nc.sync.dma_start(out=w2_raw[:, t, :], in_=w2_rows[t])
 
-        pairs = {
-            0: third.tile([P, 2 * U], F32, name="pair0", offset=0, align_bytes=ALIGN),
-            2: sbuf([P, 2 * U], F32, "pair2"),
-        }
-        windows = dict(pairs)
-        windows[3] = sbuf([P, U], F32, "window3")
-        windows[1] = shared.tile([P, U], F32, name="window1", offset=0, align_bytes=ALIGN)
+        windows = {t: sbuf([P, U], F32, "window%d" % t) for t in range(PACK)}
         zero = sbuf([P, 1], F32, "zero")
         nc.vector.memset(zero[:], 0.0)
-        for t in (3, 1):
+        nc.scalar.activation(out=windows[1][:], in_=zero[:].to_broadcast([P, U]), func=COPY)
+        for t in (2, 3, 0):
             nc.vector.memset(windows[t][:], 0.0)
-        for t in (2, 0):
-            nc.scalar.copy(out=windows[t][:, 0:U], in_=zero[:].to_broadcast([P, U]))
 
         picked_scales = sbuf([P, S], U8, "picked_scales")
         nc.vector.tensor_copy(picked_scales[:], scale_table[:].indirect(offs_t[:]))
-        skip_scales, skip_words = {}, {}
+        skip_scales = {}
 
-        def gather_skip(store, table, dtype, first, count, after=None):
-            tile = sbuf([P, count], dtype, "skip%d_%d" % (store is skip_words, first), after=after)
-            nc.vector.tensor_copy(tile[:], table[:].indirect(entries(skip_t, first, count)))
-            for c0 in range(first, first + count, CHUNK):
-                store[c0] = tile[:, c0 - first : count]
+        def gather_skip_scales(first, count, after=None):
+            tile = sbuf([P, count], U8, "skip_scales%d" % first, after=after)
+            nc.vector.tensor_copy(tile[:], scale_table[:].indirect(entries(skip_t, first, count)))
+            for c0 in range(0, count, CHUNK):
+                skip_scales[(first + c0) // CHUNK] = tile[:, c0:count]
 
-        gather_skip(skip_scales, scale_table, U8, 0, LATE)
+        gather_skip_scales(0, LATE)
+        skip_words = {}
+
+        def gather_skip(c, chunks=1, after=None):
+            tile = sbuf([P, chunks * CHUNK], U32, "skip_words%d" % c, after=after)
+            nc.vector.tensor_copy(tile[:], word_table[:].indirect(entries(skip_t, c * CHUNK, chunks * CHUNK)))
+            for k in range(chunks):
+                skip_words[c + k] = tile[:, k * CHUNK : chunks * CHUNK]
 
         w1_planes = w1_raw[:].rearrange("p (j b t h i) -> p t b h j i", j=PACK, t=PACK, h=2, i=4)
         w1_codes, w1_scales = {}, {}
@@ -151,143 +147,138 @@ def tile_picked_segunpool_none_p_kernel(
                 w1_codes[t], w1_scales[t] = codes[:, cols], scales[:, cols]
             quantize(codes[:], scales[:], grouped[:])
 
-        def project(t, first, count, b, y=None):
+        def project(t, first, count, b):
             picked = slice(first, first + count)
             bank = bank_tile(b, "y_bank%d_%d" % (t, first))
             product(bank[:, 0:count], w1_codes[t], w1_scales[t], 0, picked_words[:, picked], picked_scales[:, picked], True, True)
-            if y is None:
-                y = sbuf([P, count], F32, "y%d_%d" % (t, first))[:]
-            nc.scalar.copy(out=y, in_=bank[:, 0:count])
-            return y
+            return bank
 
-        def scatter(t, y, first, count):
-            nc.vector.tensor_copy(windows[t][:].indirect(entries(where_t, first, count)), y)
+        def vector_scatter(t, first, count):
+            nc.vector.tensor_copy(windows[t][:].indirect(entries(where_t, first, count)), y[t][:, first : first + count])
 
-        def pair_rows(t):
-            return pairs[t][:].rearrange("p (t w) -> p t w", t=2)
+        def scalar_scatter(t, first, count):
+            window = windows[t][:].indirect(entries(where_t, first, count))
+            nc.scalar.activation(out=window, in_=y[t][:, first : first + count], func=COPY)
 
-        quantize_w1((3, 1))
+        def move(copy, t, first, stop):
+            copy(out=planes_row[:, t * U + first : t * U + stop], in_=windows[t][:, first:stop])
+
+        quantize_w1((2, 3))
         picked_words = sbuf([P, S], U32, "picked_words")
         for first in (0, HALF):
             nc.vector.tensor_copy(picked_words[:, first : first + HALF], word_table[:].indirect(entries(offs_t, first, HALF)))
-        quantize_w1((2, 0), after="w1_grouped3")
-        y3 = sbuf([P, S], F32, "y3")
-        project(3, 0, HALF, 4, y=y3[:, 0:HALF])
-        project(3, HALF, HALF, 5, y=y3[:, HALF:S])
-        gather_skip(skip_words, word_table, U32, 0, WIDE)
-        scatter(3, y3[:], 0, S)
-        nc.sync.dma_start(out=pairs[2][:, U : 2 * U], in_=windows[3][:])
-        y1 = project(1, 0, S, 3)
-        scatter(1, y1, 0, S)
-        nc.sync.dma_start(out=pairs[0][:, U : 2 * U], in_=windows[1][:])
-        y2 = project(2, 0, S, 6)
-        y0_bank = bank_tile(7, "y_bank0")
-        product(y0_bank[:], w1_codes[0], w1_scales[0], 0, picked_words[:], picked_scales[:], True, True)
-        y0_low = sbuf([P, SPLIT], F32, "y0_low")
-        nc.scalar.copy(out=y0_low[:], in_=y0_bank[:, 0:SPLIT])
+        quantize_w1((0, 1), after="w1_grouped2")
+        planes_row = sbuf([P, PACK * U], F32, "planes")
+        planes = planes_row[:].rearrange("p (t w) -> p t w", t=PACK)
+        y = {t: sbuf([P, S], F32, "y%d" % t) for t in (2, 3)}
+        for n, (first, t) in enumerate(((0, 3), (0, 2), (HALF, 3), (HALF, 2))):
+            bank = project(t, first, HALF, (6, 7, 4, 5)[n])
+            nc.scalar.copy(out=y[t][:, first : first + HALF], in_=bank[:, 0:HALF])
+        gather_skip(0, 2)
+        gather_skip_scales(LATE, CHUNK, after="w1_raw")
+        scalar_scatter(3, 0, S)
+        move(nc.sync.dma_start, 3, 0, U)
+        vector_scatter(2, 0, S)
+        move(nc.sync.dma_start, 2, 0, U)
+        late_banks = {t: project(t, 0, S, b) for t, b in ((0, 6), (1, 7))}
+        for t in (0, 1):
+            y[t] = sbuf([P, S], F32, "y%d" % t)
+        for t, first, stop in ((0, 0, SPLIT), (1, 0, S), (0, SPLIT, S)):
+            nc.scalar.copy(out=y[t][:, first:stop], in_=late_banks[t][:, first:stop])
+        vector_scatter(0, 0, SPLIT)
+        scalar_scatter(1, 0, S)
+        scalar_scatter(0, SPLIT, S - SPLIT)
 
-        w3_grouped = sbuf([P, N, PACK], BF16, "w3_grouped", after="w1_codes2")
-        interleave(nc.scalar.copy, w3_grouped[:], w3_raw[:])
-        w2_grouped = sbuf([P, N, PACK], BF16, "w2_grouped", after="y3")
-        interleave(nc.scalar.copy, w2_grouped[:], w2_raw[:])
+        def gpsimd_copy(out, in_):
+            nc.gpsimd.tensor_scalar(out, in_, 1.0, 0.0, MULT, ADD)
 
-        scatter(2, y2, 0, S)
-        y0_high = shared.tile([P, S - SPLIT], F32, name="y0_high", offset=N, align_bytes=ALIGN)
-        nc.scalar.copy(out=y0_high[:], in_=y0_bank[:, SPLIT:S])
-        grouped = {}
-        for c0, cols in CHUNKS:
-            grouped[c0] = sbuf([P, cols, PACK], BF16, "z_grouped%d" % c0)[:]
-            interleave(nc.scalar.copy, grouped[c0][:, :, 2:4], pair_rows(2)[:, :, c0 : c0 + cols])
-        scatter(0, y0_low[:], 0, SPLIT)
-        w3_codes = sbuf([P, N], U32, "w3_codes")
-        w3_scales = shared.tile([P, N], U8, name="w3_scales", offset=0, align_bytes=ALIGN)
-        quantize(w3_codes[:], w3_scales[:], w3_grouped[:])
-        scatter(0, y0_high[:], SPLIT, S - SPLIT)
-        w2_codes = sbuf([P, N], U32, "w2_codes")
-        w2_scales = sbuf([P, N], U8, "w2_scales", after="y0_low")
-        quantize(w2_codes[:], w2_scales[:], w2_grouped[:])
+        def quantize_weight(grouped, name):
+            codes = sbuf([P, N], U32, name + "_codes")
+            scales = sbuf([P, N], U8, name + "_scales")
+            quantize(codes[:], scales[:], grouped)
+            return codes, scales
+
+        w3_grouped = sbuf([P, N, PACK], BF16, "w3_grouped", after="w1_grouped2")[:]
+        w2_grouped = planes_row[:, P : P + U].bitcast(BF16).rearrange("p (c j) -> p c j", j=PACK)
+        for grouped, raw in ((w3_grouped, w3_raw), (w2_grouped, w2_raw)):
+            nc.gpsimd.tensor_scalar(grouped, raw[:].rearrange("p j c -> p c j"), 1.0, 0.0, MULT, ADD)
+        w3_codes, w3_scales = quantize_weight(w3_grouped, "w3")
+        w2_codes, w2_scales = quantize_weight(w2_grouped, "w2")
+        gather_skip(2, after="w2_raw")
+        move(nc.vector.tensor_copy, 1, 0, U)
+        move(nc.vector.tensor_copy, 0, 0, CHUNK)
+        move(nc.vector.tensor_copy, 0, CHUNK, U)
 
         out_tiles = out.rearrange("(m p) w -> p m w", p=P)
-        banks, passes_left = {}, {}
+        banks, passes_left, results = {}, {}, {}
 
-        def add(n, c, chunks, w_codes, w_scales, codes, scales):
-            m, first, count, b = STORES[n]
-            opens = n not in banks
-            if opens:
-                banks[n] = bank_tile(b, "out_bank%d" % n)
-                passes_left[n] = 2 * count
-            passes_left[n] = passes_left[n] - chunks
-            at, cols = (c - first) * CHUNK, chunks * CHUNK
-            product(
-                banks[n][:, at : at + cols], w_codes, w_scales, m,
-                codes[:, 0:cols], scales[:, 0:cols], opens, passes_left[n] == 0,
-            )
-
-        def stores_with(c):
-            return [n for n, (m, first, count, b) in enumerate(STORES) if first <= c < first + count]
-
-        def skip_product(n, c, chunks=1):
-            add(n, c, chunks, w3_codes, w3_scales, skip_words[c * CHUNK], skip_scales[c * CHUNK])
-
-        def z_product(n, c, chunks=1):
-            add(n, c, chunks, w2_codes, w2_scales, z_codes[c], z_scales[:, c * CHUNK : U])
-
-        def low_pair(copy, c0, first, stop):
-            interleave(copy, grouped[c0][:, first:stop, 0:2], pair_rows(0)[:, :, c0 + first : c0 + stop])
-
-        early_codes = sbuf([P, LATE], U32, "early_codes")
-        late_codes = sbuf([P, CHUNK], U32, "late_codes", after=4)
-        z_codes = [early_codes[:, c0:LATE] for c0 in range(0, LATE, CHUNK)] + [late_codes[:]]
-        z_scales = sbuf([P, U], U8, "z_scales")
-
-        def quantize_z(c):
-            cols = slice(c * CHUNK, (c + 1) * CHUNK)
-            quantize(z_codes[c][:, 0:CHUNK], z_scales[:, cols], grouped[c * CHUNK])
-
-        results = {}
+        def add(chunks, w_codes, w_scales, codes, scales):
+            for n, (b, pieces) in enumerate(STORES):
+                mine = [k for k, (m, c) in enumerate(pieces) if c in chunks]
+                runs = [mine] if len(set(pieces[k][0] for k in mine)) == 1 else [[k] for k in mine]
+                for run in runs:
+                    m, c = pieces[run[0]]
+                    opens = n not in banks
+                    if opens:
+                        banks[n] = bank_tile(b, "out_bank%d" % n)
+                        passes_left[n] = 2 * len(pieces)
+                    passes_left[n] = passes_left[n] - len(run)
+                    closes = passes_left[n] == 0
+                    at, cols = run[0] * CHUNK, len(run) * CHUNK
+                    product(banks[n][:, at : at + cols], w_codes, w_scales, m, codes[c][:, 0:cols], scales[c][:, 0:cols], opens, closes)
+                    if closes and n != HELD_STORE:
+                        store(n)
 
         def store(n):
-            m, first, count, b = STORES[n]
-            cols = count * CHUNK
-            result = sbuf([P, cols], F32, "result%d" % n, after=VECTOR_STORES.get(n))
+            b, pieces = STORES[n]
+            cols = len(pieces) * CHUNK
+            result = sbuf([P, cols], F32, "result%d" % n)
+            results[n] = result
             copy = nc.vector.tensor_copy if n in VECTOR_STORES else nc.scalar.copy
             copy(out=result[:], in_=banks[n][:, 0:cols])
-            results[n] = result
-            queue = nc.scalar if n in VECTOR_STORES else nc.sync
-            queue.dma_start(out=out_tiles[:, m, first * CHUNK : first * CHUNK + cols], in_=result[:])
+            m, c = pieces[0]
+            if pieces[-1][0] == m:
+                nc.sync.dma_start(out=out_tiles[:, m, c * CHUNK : c * CHUNK + cols], in_=result[:])
+            else:
+                nc.sync.dma_start(
+                    out=out_tiles[:, m : m + 2, c * CHUNK : (c + 1) * CHUNK],
+                    in_=result[:].rearrange("p (m w) -> p m w", m=2),
+                )
 
-        for n, (m, first, count, b) in enumerate(STORES):
-            if first < 2:
-                skip_product(n, first, min(count, 2 - first))
-        low_pair(nc.vector.tensor_copy, 0, 0, CHUNK)
-        low_pair(nc.vector.tensor_copy, LATE, 0, SHARE)
-        low_pair(nc.scalar.copy, CHUNK, 0, CHUNK)
-        low_pair(nc.scalar.copy, WIDE, 0, CHUNK)
-        low_pair(nc.scalar.copy, LATE, SHARE, CHUNK)
-        for c in (0, 1, 2):
+        def skip_products(*chunks):
+            add(chunks, w3_codes, w3_scales, skip_words, skip_scales)
+
+        grouped, z_codes, z_scales = {}, {}, {}
+
+        def lay_out(copy, c, first=0, stop=CHUNK):
+            if c not in grouped:
+                grouped[c] = sbuf([P, CHUNK, PACK], BF16, "z_grouped%d" % c, after=(1, 4, 2, 5)[c])
+            interleave(copy, grouped[c][:, first:stop, :], planes[:, :, c * CHUNK + first : c * CHUNK + stop])
+
+        def quantize_z(c):
+            codes = sbuf([P, CHUNK], U32, "z_codes%d" % c)
+            scales = sbuf([P, CHUNK], U8, "z_scales%d" % c)
+            quantize(codes[:], scales[:], grouped[c][:])
+            z_codes[c], z_scales[c] = codes[:], scales[:]
+
+        def z_products(c):
+            add((c,), w2_codes, w2_scales, z_codes, z_scales)
+
+        skip_products(0, 1)
+        lay_out(nc.vector.tensor_copy, 0, 0, CHUNK // 2)
+        lay_out(nc.scalar.copy, 0, CHUNK // 2, CHUNK)
+        lay_out(nc.scalar.copy, 1, 0, 3 * CHUNK // 4)
+        lay_out(nc.vector.tensor_copy, 1, 3 * CHUNK // 4, CHUNK)
+        for c in (0, 1):
             quantize_z(c)
-        for n in (0, 1):
-            z_product(n, 0)
-            store(n)
-        z_product(2, 0)
-        z_product(2, 1)
-        store(2)
-        z_product(3, 0, 2)
-        store(3)
-        for n in (4, 5):
-            z_product(n, 1)
-        gather_skip(skip_words, word_table, U32, WIDE, CHUNK, after=1)
+            z_products(c)
+        skip_products(2)
+        lay_out(nc.vector.tensor_copy, 2)
+        quantize_z(2)
+        z_products(2)
+        lay_out(nc.vector.tensor_copy, 3)
+        gather_skip(3, after=4)
+        skip_products(3)
         quantize_z(3)
-        gather_skip(skip_scales, scale_table, U8, LATE, CHUNK, after=2)
-        gather_skip(skip_words, word_table, U32, LATE, CHUNK, after=3)
-        for n in stores_with(2):
-            z_product(n, 2)
-        for n in stores_with(2):
-            skip_product(n, 2)
-            if passes_left[n] == 0:
-                store(n)
-        for n in stores_with(3):
-            z_product(n, 3)
-        for n in stores_with(3):
-            skip_product(n, 3)
-            store(n)
+        store(HELD_STORE)
+        z_products(3)

@@ -27,9 +27,9 @@ SPLIT = 384
 LATE = U - CHUNK
 STORES = (
     (0, ((0, 0),)), (1, ((1, 0),)), (2, ((2, 0), (3, 0))), (3, ((0, 1), (1, 1))), (4, ((2, 1), (3, 1))),
-    (5, ((0, 2), (1, 2))), (0, ((2, 2), (3, 2))), (6, ((0, 3), (1, 3))), (7, ((2, 3), (3, 3))),
+    (5, ((0, 2), (1, 2))), (0, ((2, 2), (3, 2))), (6, ((0, 3),)), (7, ((1, 3),)), (1, ((2, 3),)), (2, ((3, 3),)),
 )
-VECTOR_STORES = (6, 8)
+VECTOR_STORES = (6, 8, 10)
 HELD_STORE = 6
 
 
@@ -39,8 +39,8 @@ def entries(list_tile, first, count):
 
 def interleave(copy, grouped, rows):
     copy(
-        out=grouped.rearrange("p (c i) j -> p c j i", i=2),
-        in_=rows.rearrange("p j (c i) -> p c j i", i=2),
+        out=grouped.rearrange("p (c i) j -> p c j i", i=4),
+        in_=rows.rearrange("p j (c i) -> p c j i", i=4),
     )
 
 

@@ -23,7 +23,7 @@ BANK_COLS = 512
 HALF = S // 2
 CHUNK = 256
 EARLY = 704
-SPLIT = 384
+SPLIT = 448
 LATE = U - CHUNK
 STORES = (
     (0, ((0, 0),)), (1, ((1, 0),)), (2, ((2, 0), (3, 0))), (3, ((0, 1), (1, 1))), (4, ((2, 1), (3, 1))),

@@ -175,7 +175,6 @@ def tile_picked_segunpool_none_p_kernel(
             bank = project(t, first, HALF, (6, 7, 4, 5)[n])
             nc.scalar.copy(out=y[t][:, first : first + HALF], in_=bank[:, 0:HALF])
         gather_skip(0, 2)
-        gather_skip_scales(LATE, CHUNK, after="w1_raw")
         scalar_scatter(3, 0, S)
         move(nc.sync.dma_start, 3, 0, U)
         vector_scatter(2, 0, S)
@@ -192,8 +191,8 @@ def tile_picked_segunpool_none_p_kernel(
         def gpsimd_copy(out, in_):
             nc.gpsimd.tensor_scalar(out, in_, 1.0, 0.0, MULT, ADD)
 
-        def quantize_weight(grouped, name):
-            codes = sbuf([P, N], U32, name + "_codes")
+        def quantize_weight(grouped, name, after=None):
+            codes = sbuf([P, N], U32, name + "_codes", after=after)
             scales = sbuf([P, N], U8, name + "_scales")
             quantize(codes[:], scales[:], grouped)
             return codes, scales
@@ -202,9 +201,8 @@ def tile_picked_segunpool_none_p_kernel(
         w2_grouped = planes_row[:, P : P + U].bitcast(BF16).rearrange("p (c j) -> p c j", j=PACK)
         for grouped, raw in ((w3_grouped, w3_raw), (w2_grouped, w2_raw)):
             nc.gpsimd.tensor_scalar(grouped, raw[:].rearrange("p j c -> p c j"), 1.0, 0.0, MULT, ADD)
-        w3_codes, w3_scales = quantize_weight(w3_grouped, "w3")
         w2_codes, w2_scales = quantize_weight(w2_grouped, "w2")
-        gather_skip(2, after="w2_raw")
+        w3_codes, w3_scales = quantize_weight(w3_grouped, "w3", after="w2_raw")
         move(nc.vector.tensor_copy, 1, 0, U)
         move(nc.vector.tensor_copy, 0, 0, CHUNK)
         move(nc.vector.tensor_copy, 0, CHUNK, U)
@@ -252,7 +250,7 @@ def tile_picked_segunpool_none_p_kernel(
 
         def lay_out(copy, c, first=0, stop=CHUNK):
             if c not in grouped:
-                grouped[c] = sbuf([P, CHUNK, PACK], BF16, "z_grouped%d" % c, after=(1, 4, 2, 5)[c])
+                grouped[c] = sbuf([P, CHUNK, PACK], BF16, "z_grouped%d" % c, after=(1, 4, 2, 1)[c])
             interleave(copy, grouped[c][:, first:stop, :], planes[:, :, c * CHUNK + first : c * CHUNK + stop])
 
         def quantize_z(c):
@@ -267,17 +265,21 @@ def tile_picked_segunpool_none_p_kernel(
         skip_products(0, 1)
         lay_out(nc.vector.tensor_copy, 0, 0, CHUNK // 2)
         lay_out(nc.scalar.copy, 0, CHUNK // 2, CHUNK)
-        lay_out(nc.scalar.copy, 1, 0, 3 * CHUNK // 4)
-        lay_out(nc.vector.tensor_copy, 1, 3 * CHUNK // 4, CHUNK)
-        for c in (0, 1):
-            quantize_z(c)
-            z_products(c)
-        skip_products(2)
+        lay_out(nc.scalar.copy, 1, 0, 5 * CHUNK // 8)
+        lay_out(nc.vector.tensor_copy, 1, 5 * CHUNK // 8, CHUNK)
+        quantize_z(0)
+        z_products(0)
         lay_out(nc.vector.tensor_copy, 2)
+        quantize_z(1)
+        z_products(1)
+        gather_skip(2, after=4)
+        skip_products(2)
         quantize_z(2)
         z_products(2)
-        lay_out(nc.vector.tensor_copy, 3)
-        gather_skip(3, after=4)
+        grouped[3] = sbuf([P, CHUNK, PACK], BF16, "z_grouped3", after=1)
+        nc.gpsimd.tensor_scalar(grouped[3][:], planes[:, :, LATE:U].rearrange("p j c -> p c j"), 1.0, 0.0, MULT, ADD)
+        gather_skip(3, after=5)
+        gather_skip_scales(LATE, CHUNK, after=3)
         skip_products(3)
         quantize_z(3)
         store(HELD_STORE)

@@ -23,7 +23,7 @@ BANK_COLS = 512
 HALF = S // 2
 CHUNK = 256
 EARLY = 704
-SPLIT = 448
+SPLIT = 416
 LATE = U - CHUNK
 STORES = (
     (0, ((0, 0),)), (1, ((1, 0),)), (2, ((2, 0), (3, 0))), (3, ((0, 1), (1, 1))), (4, ((2, 1), (3, 1))),

@@ -23,7 +23,7 @@ BANK_COLS = 512
 HALF = S // 2
 CHUNK = 256
 EARLY = 704
-SPLIT = 416
+SPLIT = 448
 LATE = U - CHUNK
 STORES = (
     (0, ((0, 0),)), (1, ((1, 0),)), (2, ((2, 0), (3, 0))), (3, ((0, 1), (1, 1))), (4, ((2, 1), (3, 1))),
@@ -203,9 +203,10 @@ def tile_picked_segunpool_none_p_kernel(
             nc.gpsimd.tensor_scalar(grouped, raw[:].rearrange("p j c -> p c j"), 1.0, 0.0, MULT, ADD)
         w2_codes, w2_scales = quantize_weight(w2_grouped, "w2")
         w3_codes, w3_scales = quantize_weight(w3_grouped, "w3", after="w2_raw")
-        move(nc.vector.tensor_copy, 1, 0, U)
+        move(nc.vector.tensor_copy, 1, 0, LATE)
         move(nc.vector.tensor_copy, 0, 0, CHUNK)
-        move(nc.vector.tensor_copy, 0, CHUNK, U)
+        move(nc.vector.tensor_copy, 0, CHUNK, LATE)
+        move(nc.sync.dma_start, 1, LATE, U)
 
         out_tiles = out.rearrange("(m p) w -> p m w", p=P)
         banks, passes_left, results = {}, {}, {}
@@ -269,6 +270,7 @@ def tile_picked_segunpool_none_p_kernel(
         lay_out(nc.vector.tensor_copy, 1, 5 * CHUNK // 8, CHUNK)
         quantize_z(0)
         z_products(0)
+        move(nc.vector.tensor_copy, 0, LATE, U)
         lay_out(nc.vector.tensor_copy, 2)
         quantize_z(1)
         z_products(1)

from contextlib import ExitStack

import concourse.mybir as mybir

K, T, S, N, U, H = 512, 2048, 512, 512, 1024, 512
FLOPS = 2 * K * H * S + 2 * H * N * U + 2 * K * N * U

F32 = mybir.dt.float32
BF16 = mybir.dt.bfloat16
I32 = mybir.dt.int32
U32 = mybir.dt.uint32
U16 = mybir.dt.uint16
U8 = mybir.dt.uint8
FP8X4 = mybir.dt.float8_e4m3fn_x4
COPY = mybir.ActivationFunctionType.Copy
MULT, ADD = mybir.AluOpType.mult, mybir.AluOpType.add

P = 128
PACK = 4
LIST_ROWS = 16
ALIGN = 64
BANK_COLS = 512
HALF = S // 2
CHUNK = 256
EARLY = 704
SPLIT = 448
LATE = U - CHUNK
STORES = (
    (0, ((0, 0),)), (1, ((1, 0),)), (2, ((2, 0), (3, 0))), (3, ((0, 1), (1, 1))), (4, ((2, 1), (3, 1))),
    (5, ((0, 2), (1, 2))), (0, ((2, 2), (3, 2))), (6, ((0, 3),)), (7, ((1, 3),)), (1, ((2, 3),)), (2, ((3, 3),)),
)
VECTOR_STORES = (6, 8, 10)
HELD_STORE = 6


def entries(list_tile, first, count):
    return list_tile[:, first // LIST_ROWS : (first + count) // LIST_ROWS]


def interleave(copy, grouped, rows):
    copy(
        out=grouped.rearrange("p (c i) j -> p c j i", i=4),
        in_=rows.rearrange("p j (c i) -> p c j i", i=4),
    )


def tile_picked_segunpool_none_p_kernel(
    tc, x_words, x_scales, w1, w2, w3, offs, where, skip, out
):
    nc = tc.nc
    with ExitStack() as ctx:
        lists = ctx.enter_context(tc.tile_pool(name="lists", bufs=1))
        keep = ctx.enter_context(tc.tile_pool(name="keep", bufs=1))
        placed = ctx.enter_context(tc.tile_pool(name="placed", bufs=1))
        psum = ctx.enter_context(tc.psum_pool(name="psum", bufs=1))

        def sbuf(shape, dtype, name, after=None):
            if isinstance(after, int):
                return placed.tile(shape, dtype, name=name, offset=after * 4 * CHUNK, align_bytes=ALIGN)
            return keep.tile(shape, dtype, name=name, tag=after or name, align_bytes=ALIGN)

        def bank_tile(b, name):
            return psum.tile([P, BANK_COLS], F32, name=name, tag="bank%d" % b)

        def quantize(codes, scales, grouped):
            nc.vector.quantize_mx(out=codes.bitcast(FP8X4), scales=scales, in_=grouped.rearrange("p c j -> p (c j)"))

        def product(acc, w_codes, w_scales, w_tile, codes, scales, start, stop):
            w_cols = slice(w_tile * P, (w_tile + 1) * P)
            nc.tensor.matmul_mx(
                out=acc,
                lhsT=w_codes[:, w_cols].bitcast(FP8X4),
                lhsT_scale=w_scales[:, w_cols],
                rhs=codes.bitcast(FP8X4),
                rhs_scale=scales,
                start=start,
                stop=stop,
            )

        scale_table = sbuf([P, T], U8, "scale_table")
        nc.vector.memset(scale_table[:].bitcast(I32), 0)
        w1_rows = w1.rearrange("(p j) c -> p (j c)", j=PACK)
        w1_raw = sbuf([P, PACK * H], F32, "w1_raw")
        nc.scalar.dma_start(out=w1_raw[:, 0:EARLY], in_=w1_rows[:, 0:EARLY])
        offs_t = lists.tile([P, S // LIST_ROWS], U16, name="offs_t")
        nc.sync.dma_start(offs_t[:], offs)
        for r in range(4):
            nc.sync.dma_start(
                out=scale_table[r:P:32, :].bitcast(I32),
                in_=x_scales[0, r:16:4, :].bitcast(I32),
            )
        skip_t = lists.tile([P, U // LIST_ROWS], U16, name="skip_t")
        nc.sync.dma_start(skip_t[:], skip)
        nc.sync.dma_start(out=w1_raw[:, EARLY : PACK * H], in_=w1_rows[:, EARLY : PACK * H])
        word_table = sbuf([P, T], U32, "word_table")
        nc.sync.dma_start(
            out=word_table[:].bitcast(I32), in_=x_words[0].rearrange("p c r -> p (c r)").bitcast(I32)
        )
        where_t = lists.tile([P, S // LIST_ROWS], U16, name="where_t")
        nc.sync.dma_start(where_t[:], where)
        w3_raw = sbuf([P, PACK, N], F32, "w3_raw")
        nc.sync.dma_start(out=w3_raw[:], in_=w3.rearrange("(p j) c -> p j c", j=PACK))
        w2_raw = sbuf([P, PACK, N], F32, "w2_raw")
        w2_rows = w2.rearrange("(b t q) c -> t b q c", t=PACK, q=8)
        for t in range(PACK):
            nc.sync.dma_start(out=w2_raw[:, t, :], in_=w2_rows[t])

        windows = {t: sbuf([P, U], F32, "window%d" % t) for t in range(PACK)}
        zero = sbuf([P, 1], F32, "zero")
        nc.vector.memset(zero[:], 0.0)
        nc.scalar.activation(out=windows[1][:], in_=zero[:].to_broadcast([P, U]), func=COPY)
        for t in (2, 3, 0):
            nc.vector.memset(windows[t][:], 0.0)

        picked_scales = sbuf([P, S], U8, "picked_scales")
        nc.vector.tensor_copy(picked_scales[:], scale_table[:].indirect(offs_t[:]))
        skip_scales = {}

        def gather_skip_scales(first, count, after=None):
            tile = sbuf([P, count], U8, "skip_scales%d" % first, after=after)
            nc.vector.tensor_copy(tile[:], scale_table[:].indirect(entries(skip_t, first, count)))
            for c0 in range(0, count, CHUNK):
                skip_scales[(first + c0) // CHUNK] = tile[:, c0:count]

        gather_skip_scales(0, LATE)
        skip_words = {}

        def gather_skip(c, chunks=1, after=None):
            tile = sbuf([P, chunks * CHUNK], U32, "skip_words%d" % c, after=after)
            nc.vector.tensor_copy(tile[:], word_table[:].indirect(entries(skip_t, c * CHUNK, chunks * CHUNK)))
            for k in range(chunks):
                skip_words[c + k] = tile[:, k * CHUNK : chunks * CHUNK]

        w1_planes = w1_raw[:].rearrange("p (j b t h i) -> p t b h j i", j=PACK, t=PACK, h=2, i=4)
        w1_codes, w1_scales = {}, {}

        def quantize_w1(ts, after=None):
            name = "%d" % ts[0]
            grouped = sbuf([P, len(ts) * P, PACK], BF16, "w1_grouped" + name, after=after)
            codes = sbuf([P, len(ts) * P], U32, "w1_codes" + name)
            scales = sbuf([P, len(ts) * P], U8, "w1_scales" + name)
            for n, t in enumerate(ts):
                cols = slice(n * P, (n + 1) * P)
                nc.scalar.copy(
                    out=grouped[:, cols, :].rearrange("p (b h i) j -> p b h j i", h=2, i=4), in_=w1_planes[:, t]
                )
                w1_codes[t], w1_scales[t] = codes[:, cols], scales[:, cols]
            quantize(codes[:], scales[:], grouped[:])

        def project(t, first, count, b):
            picked = slice(first, first + count)
            bank = bank_tile(b, "y_bank%d_%d" % (t, first))
            product(bank[:, 0:count], w1_codes[t], w1_scales[t], 0, picked_words[:, picked], picked_scales[:, picked], True, True)
            return bank

        def vector_scatter(t, first, count):
            nc.vector.tensor_copy(windows[t][:].indirect(entries(where_t, first, count)), y[t][:, first : first + count])

        def scalar_scatter(t, first, count):
            window = windows[t][:].indirect(entries(where_t, first, count))
            nc.scalar.activation(out=window, in_=y[t][:, first : first + count], func=COPY)

        def move(copy, t, first, stop):
            copy(out=planes_row[:, t * U + first : t * U + stop], in_=windows[t][:, first:stop])

        quantize_w1((2, 3))
        picked_words = sbuf([P, S], U32, "picked_words")
        for first in (0, HALF):
            nc.vector.tensor_copy(picked_words[:, first : first + HALF], word_table[:].indirect(entries(offs_t, first, HALF)))
        quantize_w1((0, 1), after="w1_grouped2")
        planes_row = sbuf([P, PACK * U], F32, "planes")
        planes = planes_row[:].rearrange("p (t w) -> p t w", t=PACK)
        y = {t: sbuf([P, S], F32, "y%d" % t) for t in (2, 3)}
        for n, (first, t) in enumerate(((0, 3), (0, 2), (HALF, 3), (HALF, 2))):
            bank = project(t, first, HALF, (6, 7, 4, 5)[n])
            nc.scalar.copy(out=y[t][:, first : first + HALF], in_=bank[:, 0:HALF])
        gather_skip(0, 2)
        scalar_scatter(3, 0, S)
        move(nc.sync.dma_start, 3, 0, U)
        vector_scatter(2, 0, S)
        move(nc.sync.dma_start, 2, 0, U)
        late_banks = {t: project(t, 0, S, b) for t, b in ((0, 6), (1, 7))}
        for t in (0, 1):
            y[t] = sbuf([P, S], F32, "y%d" % t)
        for t, first, stop in ((0, 0, SPLIT), (1, 0, S), (0, SPLIT, S)):
            nc.scalar.copy(out=y[t][:, first:stop], in_=late_banks[t][:, first:stop])
        vector_scatter(0, 0, SPLIT)
        scalar_scatter(1, 0, S)
        scalar_scatter(0, SPLIT, S - SPLIT)

        def gpsimd_copy(out, in_):
            nc.gpsimd.tensor_scalar(out, in_, 1.0, 0.0, MULT, ADD)

        def quantize_weight(grouped, name, after=None):
            codes = sbuf([P, N], U32, name + "_codes", after=after)
            scales = sbuf([P, N], U8, name + "_scales")
            quantize(codes[:], scales[:], grouped)
            return codes, scales

        w3_grouped = sbuf([P, N, PACK], BF16, "w3_grouped", after="w1_grouped2")[:]
        w2_grouped = planes_row[:, P : P + U].bitcast(BF16).rearrange("p (c j) -> p c j", j=PACK)
        for grouped, raw in ((w3_grouped, w3_raw), (w2_grouped, w2_raw)):
            nc.gpsimd.tensor_scalar(grouped, raw[:].rearrange("p j c -> p c j"), 1.0, 0.0, MULT, ADD)
        w2_codes, w2_scales = quantize_weight(w2_grouped, "w2")
        w3_codes, w3_scales = quantize_weight(w3_grouped, "w3", after="w2_raw")
        move(nc.vector.tensor_copy, 1, 0, LATE)
        move(nc.vector.tensor_copy, 0, 0, CHUNK)
        move(nc.vector.tensor_copy, 0, CHUNK, LATE)
        move(nc.sync.dma_start, 1, LATE, U)

        out_tiles = out.rearrange("(m p) w -> p m w", p=P)
        banks, passes_left, results = {}, {}, {}

        def add(chunks, w_codes, w_scales, codes, scales):
            for n, (b, pieces) in enumerate(STORES):
                mine = [k for k, (m, c) in enumerate(pieces) if c in chunks]
                runs = [mine] if len(set(pieces[k][0] for k in mine)) == 1 else [[k] for k in mine]
                for run in runs:
                    m, c = pieces[run[0]]
                    opens = n not in banks
                    if opens:
                        banks[n] = bank_tile(b, "out_bank%d" % n)
                        passes_left[n] = 2 * len(pieces)
                    passes_left[n] = passes_left[n] - len(run)
                    closes = passes_left[n] == 0
                    at, cols = run[0] * CHUNK, len(run) * CHUNK
                    product(banks[n][:, at : at + cols], w_codes, w_scales, m, codes[c][:, 0:cols], scales[c][:, 0:cols], opens, closes)
                    if closes and n != HELD_STORE:
                        store(n)

        def store(n):
            b, pieces = STORES[n]
            cols = len(pieces) * CHUNK
            result = sbuf([P, cols], F32, "result%d" % n)
            results[n] = result
            copy = nc.vector.tensor_copy if n in VECTOR_STORES else nc.scalar.copy
            copy(out=result[:], in_=banks[n][:, 0:cols])
            m, c = pieces[0]
            if pieces[-1][0] == m:
                nc.sync.dma_start(out=out_tiles[:, m, c * CHUNK : c * CHUNK + cols], in_=result[:])
            else:
                nc.sync.dma_start(
                    out=out_tiles[:, m : m + 2, c * CHUNK : (c + 1) * CHUNK],
                    in_=result[:].rearrange("p (m w) -> p m w", m=2),
                )

        def skip_products(*chunks):
            add(chunks, w3_codes, w3_scales, skip_words, skip_scales)

        grouped, z_codes, z_scales = {}, {}, {}

        def lay_out(copy, c, first=0, stop=CHUNK):
            if c not in grouped:
                grouped[c] = sbuf([P, CHUNK, PACK], BF16, "z_grouped%d" % c, after=(1, 4, 2, 1)[c])
            interleave(copy, grouped[c][:, first:stop, :], planes[:, :, c * CHUNK + first : c * CHUNK + stop])

        def quantize_z(c):
            codes = sbuf([P, CHUNK], U32, "z_codes%d" % c)
            scales = sbuf([P, CHUNK], U8, "z_scales%d" % c)
            quantize(codes[:], scales[:], grouped[c][:])
            z_codes[c], z_scales[c] = codes[:], scales[:]

        def z_products(c):
            add((c,), w2_codes, w2_scales, z_codes, z_scales)

        skip_products(0, 1)
        lay_out(nc.vector.tensor_copy, 0, 0, CHUNK // 2)
        lay_out(nc.scalar.copy, 0, CHUNK // 2, CHUNK)
        lay_out(nc.scalar.copy, 1, 0, 5 * CHUNK // 8)
        lay_out(nc.vector.tensor_copy, 1, 5 * CHUNK // 8, CHUNK)
        quantize_z(0)
        z_products(0)
        move(nc.vector.tensor_copy, 0, LATE, U)
        lay_out(nc.vector.tensor_copy, 2)
        quantize_z(1)
        z_products(1)
        gather_skip(2, after=4)
        skip_products(2)
        quantize_z(2)
        z_products(2)
        grouped[3] = sbuf([P, CHUNK, PACK], BF16, "z_grouped3", after=1)
        nc.gpsimd.tensor_scalar(grouped[3][:], planes[:, :, LATE:U].rearrange("p j c -> p c j"), 1.0, 0.0, MULT, ADD)
        gather_skip(3, after=5)
        gather_skip_scales(LATE, CHUNK, after=3)
        skip_products(3)
        quantize_z(3)
        store(HELD_STORE)
        z_products(3)
